import numpy as np, ml_dtypes
CORES = [24,25,26,27,28,29,30,31]
N = 8
import mx_ref
BF = ml_dtypes.bfloat16
def gcols(t, e):
    v = np.concatenate([t.reshape(8, 16, -1, 4), np.zeros((8, 16, 1, 4), BF)], axis=2)
    return np.ascontiguousarray(np.stack([v[g][:, e[g]] for g in range(8)])).reshape(128, -1)
def tile(rs):
    return np.stack(rs, axis=2).reshape(128, -1).astype(BF)
def pick(q, e):
    c = np.concatenate([q[0].reshape(128, -1, 4), np.zeros((128, 1, 4), np.uint8)], axis=1); s = np.concatenate([q[1], np.ones((16, 1), np.uint8)], axis=1)
    return (np.ascontiguousarray(c[:, e].reshape(128, -1)), np.ascontiguousarray(s[:, e]))
def join(*qs):
    return (np.concatenate([q[0] for q in qs], axis=1), np.concatenate([q[1] for q in qs], axis=1))
def put(q, e, v):
    c, s = q[0].reshape(128, -1, 4).copy(), q[1].copy(); c[:, e] = v[0].reshape(128, -1, 4); s[:, e] = v[1]
    return (c.reshape(128, -1), s)
def pk(c, s):
    return (np.ascontiguousarray(c), mx_ref.live(s))
def emit(q):
    return q[0], q[1]
def packed(v, rng):
    q = [mx_ref.quantize(np.ascontiguousarray(v[r])) for r in range(N)]
    return np.stack([a for a, b in q]), np.stack([mx_ref.plane(b, rng) for a, b in q])
def values_of_codes():
    e, c = np.zeros((128, 128, 4), np.float32), np.zeros((128, 2, 4), np.uint8)
    e[np.arange(128), np.arange(128), 0] = 1
    c[:127, :, 0] = np.arange(256).reshape(2, 128).T[:127]
    return mx_ref.matmul(mx_ref.quantize(e.reshape(128, 512).astype(BF)), (c.reshape(128, 8), np.full((16, 2), 127, np.uint8))).T.reshape(-1).astype(np.float64)
CODE_VALUE, SCALE_VALUE = values_of_codes(), 2.0 ** (np.arange(256) - 127.0)
def decode(q):
    return (CODE_VALUE[q[0]].reshape(16, 8, -1, 4) * SCALE_VALUE[q[1]][:, None, :, None] + 0.0).reshape(128, -1).astype(np.float32)
def f(rng, *shape):
    return mx_ref.flush((rng.standard_normal(shape, dtype=np.float32) * np.exp2(rng.integers(-2, 3, shape[:-1] + (1,)))).astype(BF))
def wide(rng, *shape, cols=0):
    v = rng.standard_normal(shape, dtype=np.float32) * np.exp2(rng.integers(-12, 13, shape)).astype(np.float32)
    if cols: v *= np.repeat(np.exp2(rng.integers(-cols, cols + 1, shape[:-2] + (1, shape[-1] // 4))) * (rng.random(shape[:-2] + (1, shape[-1] // 4)) > 0.0625), 4, axis=-1).astype(np.float32)
    return mx_ref.flush(v.astype(BF))
C, L, S, M, R = 384, 96, 7, 3, 3
STEP = [1, 2, 4]
def park(p):
    home = np.zeros((8, C), np.int64)
    for b in range(S): home += (p[b::16] > 0) * (M << b)
    o = np.lexsort((-(p[8::16] + np.float32(0.0)), home))
    h = np.take_along_axis(home, o, 1)
    i = np.arange(C)
    place = i + np.maximum.accumulate(h - i, axis=1)
    over = place >= C
    for g in range(8): place[g, over[g]] = np.flatnonzero(~np.isin(i, place[g]))
    gap = place + C * over - h
    e = np.lexsort((place, -gap))[:, :L]
    m = np.zeros((8, C), np.int64)
    np.put_along_axis(m, place, o, 1)
    return m, np.take_along_axis(o, e, 1), np.take_along_axis(place, e, 1)
def numbers_of(rng):
    return {"x": np.array(f(rng, N, 128, 4 * C)), "u": np.array(f(rng, N, 128, 512)), "v": np.array(f(rng, N, 128, 512))}
def weights(rng, still=[], positive=False):
    w = np.array(f(rng, N, 128, 2048)).reshape(N, 8, 16, 4, 8, 16, 4)
    if positive: w = np.abs(w.astype(np.float32)).astype(BF)
    for i in still:
        w[:, :, i] = 0
        w[:, :, :, :, :, i] = 0
    c, p = packed(w.reshape(N, 128, 2048), rng)
    return {"wc": c, "ws": p}
def signs(rng):
    return np.stack([rng.permutation(8) % 2 * 2.0 - 1.0 for r in range(N)])
def setup_inputs(rng):
    return {**numbers_of(rng), **weights(rng)}
def setup_inputs_ties(rng):
    d = numbers_of(rng)
    e = rng.permutation(N)
    x = d["x"].reshape(N, 8, 16, C, 4)
    for r in range(N):
        k = np.zeros(C, int) if r == e[0] else rng.permutation(C) % 3
        a = x[r][:, :8, :3].copy()
        a[:, :, 2] = 0
        x[r][:, :8] = a[:, :, k]
    x[e[1]] = 0
    u = d["u"].reshape(N, 8, 16, 8, 16, 4)
    k = u.copy()
    u[:, :, :, :, :9] = 0
    for g in range(8): u[:, g, :8, g, :9] = k[:, g, :8, g, :9]
    return {"x": x.reshape(N, 128, 4 * C), "u": u.reshape(N, 128, 512), "v": d["v"], **weights(rng, range(8))}
def setup_inputs_near(rng):
    d = numbers_of(rng)
    x = np.zeros((N, 8, 16, C, 4), np.float32)
    u = d["u"].reshape(N, 8, 16, 8, 16, 4)
    u[:, :, :, :, :9] = 0
    o, c = rng.permutation(N) % 4, signs(rng)
    j = np.arange(C)
    upper = j // (C // 2)
    for r in range(N):
        i = (j + rng.integers(0, C, (8, 1))) % C
        if o[r] == 3: i = i % (C // 2) * 2 + upper
        z = rng.integers(0, 1 << S, (8, 8))[np.arange(8)[:, None], i // (C // 8)]
        k = 1.0 if o[r] == 0 else 2.0 ** -30
        size = 1.0 if o[r] < 2 else 2.0 ** -4
        for b in range(S): x[r, :, b, :, 0] = np.where((z >> b) & 1, k, -k * rng.integers(0, 2, (8, C)))
        if o[r] < 2: x[r, :, 7, :, 0] = k * np.where(c[r] > 0, 1.0, -1.5)[:, None]
        if o[r] == 3: x[r, :, 7, :, 0] = (8 + upper) * 2.0 ** -33
        a = (((i // 2)[:, :, None] >> np.arange(8)) & 1) * np.exp2(np.arange(8) - 23.0) * size
        x[r, :, 8] = a[:, :, :4]
        x[r, :, 9] = a[:, :, 4:]
        if o[r] < 2:
            for g in rng.permutation(8)[:4]: x[r, g, 11, rng.integers(C), 0] = 2.0 ** 30
        x[r, :, 12:] = rng.integers(4, 8, (8, 4, C, 4)) * 2.0 ** -20 * size
        for g in range(8):
            for b in range(S): u[r, g, b, g, b, 0] = k
            u[r, g, 7, g, 8, 0] = 1.0 if o[r] < 2 else k
            u[r, g, 8:10, g, 8] = k
            u[r, g, 11, g, 8, 0] = k
    return {"x": x.reshape(N, 128, 4 * C).astype(BF), "u": u.reshape(N, 128, 512), "v": d["v"], **weights(rng, range(12), True)}
def setup_inputs_huge(rng):
    d = numbers_of(rng)
    x = 2.0 ** 30 * (0.8 + 0.2 * rng.random((N, 128, C, 4)))
    c = np.ones((N, C))
    half = int(rng.integers(2))
    for r in range(N):
        if 2 * r // N == half: c[r] = rng.permutation(C) % 2 * 2.0 - 1.0
    x *= c[:, None, :, None]
    a = 2.0 ** 30 * (1 - 0.1 * rng.random((N, 128, 8, 4))) * signs(rng)[:, None, :, None]
    u = d["u"].reshape(N, 8, 16, 8, 16, 4)
    u[:, :, :, :, :9] = 0
    u[:, :, :, :, 8] = a.astype(np.float32).astype(BF).reshape(N, 8, 16, 8, 4)
    e = (2.0 ** 30 * rng.choice([-1.0, 1.0], (N, 8, S))).astype(np.float32).astype(BF)
    for g in range(8): u[:, g, :, g, :S] = e[:, g][:, None, :, None]
    w = np.zeros((N, 128, 4, 128, 4), np.float32)
    i = np.arange(128)
    for b in range(4): w[:, i, b, i, b] = -1
    wc, ws = packed(w.reshape(N, 128, 2048).astype(BF), rng)
    return {"x": x.astype(np.float32).reshape(N, 128, 4 * C).astype(BF), "u": u.reshape(N, 128, 512), "v": d["v"], "wc": wc, "ws": ws}
def setup_inputs_homes(rng):
    d = numbers_of(rng)
    x = d["x"].astype(np.float32).reshape(N, 8, 16, C, 4)
    u = d["u"].reshape(N, 8, 16, 8, 16, 4)
    x[:, :, :8] = 0
    u[:, :, :, :, :S] = 0
    last = (1 << S) - 1
    small = rng.permutation(N) < N // 2
    for r in range(N):
        k = 2.0 ** -30 if small[r] else 1.0
        one = np.arange(C) // M
        one[rng.integers(C - M)] = last
        case = [np.zeros(C, int), np.full(C, last), np.arange(C) // M, one, np.arange(C) // (C // 2) * last, np.full(C, rng.integers(last + 1))]
        for n in (L, L + 1): case.append(np.concatenate([np.arange(C - M - n) // M, np.full(M + n, last)]))
        o = rng.permutation(8)
        x[r, :, 7, :, 0] = -k
        for g in range(8):
            z = rng.permutation(case[o[g]])
            for b in range(S):
                x[r, g, b, :, 0] = k * np.where((z >> b) & 1, 1.125, rng.integers(0, 2, C))
                u[r, g, b, g, b, 0] = k
                u[r, g, 7, g, b, 0] = k
    return {"x": x.reshape(N, 128, 4 * C).astype(BF), "u": u.reshape(N, 128, 512), "v": d["v"], **weights(rng, range(8))}
def setup_inputs_spread(rng):
    d = setup_inputs(rng)
    d["x"] = wide(rng, N, 128, 4 * C, cols=6)
    return d
def check_inputs(d):
    b = []
    for k in ("x", "u", "v"):
        a = np.abs(d[k].astype(np.float32))
        if not (np.isfinite(a).all() and ((a == 0) | (a >= 2.0 ** -30) & (a <= 2.0 ** 30)).all()): b.append("a value of " + k)
    if ((d["wc"] & 0x7F) == 0x7F).any(): b.append("a code of wc that is no number")
    z = np.zeros((128, 4, 4), np.float32)
    z[:, 1] = 2.0 ** -30
    z[:, 2] = 2.0 ** 30
    c, s = emit(mx_ref.quantize(z.reshape(128, 16).astype(BF)))
    for r in range(N):
        p = mx_ref.live(d["ws"][r])
        if not ((p == s[0, 0]) | (p >= s[0, 1]) & (p <= s[0, 2])).all(): b.append("a scale of ws")
    return b
def reference(x, u, v, wc, ws):
    qu = [mx_ref.quantize(u[r]) for r in range(N)]
    lay = [pk(wc[r], ws[r]) for r in range(N)]
    now = [x[r] for r in range(N)]
    for t in range(R):
        sent, m = [], []
        for r in range(N):
            e, b, a = park(mx_ref.matmul(qu[r], mx_ref.quantize(now[r])))
            sent.append(mx_ref.quantize(gcols(now[r], b)))
            np.put_along_axis(e, a, np.tile(C + np.arange(L), (8, 1)), 1)
            m.append(e)
        made = []
        for r in range(N):
            came = decode(sent[(r - STEP[t]) % N]).astype(BF)
            c = gcols(np.concatenate([now[r], came], axis=1), m[r])
            q = mx_ref.quantize(c)
            made.append(tile([mx_ref.matmul(pick(lay[r], np.arange(128 * b, 128 * b + 128)), q) * np.float32(0.015625) + c[:, b::4].astype(np.float32) for b in range(4)]))
        now = made
    y, ot = np.zeros((N, 128, C), np.float32), np.zeros((N, 8, C), np.float32)
    oc, osc = np.zeros((N, 128, 4 * C), np.uint8), np.zeros((N, 16, C), np.uint8)
    for r in range(N):
        q = mx_ref.quantize(now[r])
        y[r] = mx_ref.matmul(mx_ref.quantize(v[r]), q)
        ot[r] = m[r]
        oc[r], osc[r] = emit(q)
    return {"y": y, "ot": ot, "oc": oc, "osc": osc}

@@ -1,0 +1,427 @@
+from concourse.mybir import dt, AluOpType, AxisListType, ActivationFunctionType
+
+A = AluOpType
+F = ActivationFunctionType
+C, L, R = 384, 96, 3
+STEP = [1, 2, 4]
+X4 = "float8_e4m3fn_x4"
+B = float(2 ** 20)
+BC = float(2 ** 42)
+EMPTY = float(2 ** 32)
+MAGIC = 1.5 * 2 ** 33
+NV = [4, 6, 6]
+WIDTH = [128] * 8 + [192] * 4 + [256] * 4 + [320] * 4 + [384] * 4
+
+SCRATCH = {}
+
+
+def _sb(name, n, dtype):
+    SCRATCH[name] = ("sbuf", [128, n], dtype)
+
+
+for _n, _w in dict(mask=C, nmask=C, mp=C, mc=2 * C, m4=L, m4a=L, cols=16, pw=32, iok=C, iop=480, k3c=C, tab2=2 * C,
+                   c1k=C, mk=C, sw=C, brow=C, prow=C, hw=C, sm=24 * 16, colw=320, krow=C,
+                   ps=C, qs=C, qw=C, xw=2 * C, y48=48, tr1=2 * C, tr2=2 * C, grow=C, k3=C, k3s=C,
+                   bl=C, b4=L, gw=C, tmp=4 * C, yo=C, otr=C).items():
+    _sb(_n, _w, "float32")
+for _n, _w in dict(vi=C, va=C, pki=16, wi=512, wsh=512, v4=L, v4a=L, si=24 * 4).items():
+    _sb(_n, _w, "int32")
+for _n, _w in dict(pko=8, o1=24, o2=24, oq=24, ol=24, o3=24, ov=96, oo=24).items():
+    _sb(_n, _w, "uint16")
+for _n, _w in dict(ut=512, vt=512, wt=1536, ones=512, et=2048, sg=C, hb=4 * C, junk=1024, sj=8 * 192, dw=4 * C, vv=4 * C,
+                   v64=4 * C, tf=4 * C, c2=768, c3=1024, c4=1280, c5=1536).items():
+    _sb(_n, _w, "bfloat16")
+for _n, _w in dict(u=128, us=128, v=128, lay=512, k=384, e=512, h=C, m=C, f=C, d2=128, d3=192, d4=256, d5=320).items():
+    _sb("Q" + _n, _w, X4)
+    _sb("Z" + _n, _w, "uint8")
+for _r in range(R):
+    _sb("wn%d" % _r, 4 * (C + L), "bfloat16")
+    _sb("xt%d" % _r, 3 * C, "float32")
+    for _n in ("t", "l"):
+        _sb("Q%s%d" % (_n, _r), C, X4)
+        _sb("Z%s%d" % (_n, _r), C, "uint8")
+    _sb("ob%d" % _r, 24, "uint16")
+    _sb("oa%d" % _r, 24, "uint16")
+for _b in range(8):
+    SCRATCH["p%d" % _b] = ("psum", [128, 512], "float32")
+
+BANKS = ["p%d" % b for b in range(8)]
+DMAS = ["dx", "du", "dv", "dwc", "dws", "dot", "doa", "dob"]
+SEMAPHORES = ["V", "S", "P", "G", "snt"] + DMAS + ["aq%d" % r for r in range(R)] + ["ao%d" % r for r in range(R)]
+
+
+def _emit(g, T, ops):
+    queue = {"V": g.vector, "S": g.scalar, "P": g.tensor, "G": g, "Y": g.sync}
+    count, writer, readers = {}, {}, {}
+    known = {q: {} for q in queue}
+    for q, sem, inc, fn, reads, writes in ops:
+        deps = []
+        for x in reads:
+            if x in writer:
+                deps.append(writer[x])
+        for x in writes:
+            if x in writer and not (x in BANKS and writer[x][0] == q):
+                deps.append(writer[x])
+            deps.extend(readers.get(x, []))
+        if fn is not None:
+            need = {}
+            for s, k, clock in deps:
+                if known[q].get(s, 0) < k and need.get(s, (0, None))[0] < k:
+                    need[s] = (k, clock)
+            for s in sorted(need, key=lambda s: -sum(need[s][1].values())):
+                k, clock = need[s]
+                if known[q].get(s, 0) >= k:
+                    continue
+                queue[q].wait_ge(T.sem[s], k)
+                known[q][s] = k
+                for s2, k2 in clock.items():
+                    if known[q].get(s2, 0) < k2:
+                        known[q][s2] = k2
+            ins = fn(queue[q])
+            if sem != "snt":
+                ins.then_inc(T.sem[sem], inc)
+        count[sem] = count.get(sem, 0) + inc
+        if sem == "snt":
+            continue
+        me = (sem, count[sem], dict(known[q]) if fn is not None else {})
+        for x in reads:
+            readers.setdefault(x, []).append(me)
+        for x in writes:
+            writer[x] = me
+            readers[x] = []
+    for s in sorted(count):
+        g.wait_ge(T.sem[s], count[s])
+
+
+def rank_program(g, core, T, topo):
+    rank = T.rank_of(core)
+    if rank is None:
+        return
+    n = len(T.cores)
+    ops = []
+
+    def op(q, fn, reads, writes):
+        ops.append((q, q, 1, fn, reads, writes))
+
+    def dma(q, sem, out, in_, reads, writes):
+        ops.append((q, sem, 16, lambda e: e.dma_start(out, in_), reads, writes))
+
+    def send(dst, sem, out, in_, reads):
+        rid, pid, _ = topo.addr(dst)
+        m = topo.mask(core, dst)
+        ops.append(("G", "snt", len(topo.engines(core, dst)),
+                    lambda e: e.remote_dma(out, in_, T.sem[sem], T.sem.snt, pid, rid, m), reads, []))
+
+    def arrive(src, sem, k, writes):
+        ops.append(("G", sem, k * len(topo.engines(src, core)), None, [], writes))
+
+    def ts(out, in0, s1, s2, op0, op1, reads, writes):
+        if op1 is None:
+            op("V", lambda e: e.tensor_scalar(out, in0, s1, None, op0), reads, writes)
+        else:
+            op("V", lambda e: e.tensor_scalar(out, in0, s1, s2, op0, op1), reads, writes)
+
+    def tt(out, in0, in1, o, reads, writes):
+        op("V", lambda e: e.tensor_tensor(out, in0, in1, o), reads, writes)
+
+    def cp(out, in_, reads, writes):
+        op("V", lambda e: e.tensor_copy(out, in_), reads, writes)
+
+    def scan(out, d0, d1, init, op0, op1, reads, writes):
+        op("V", lambda e: e.tensor_tensor_scan(out, d0, d1, init, op0, op1), reads, writes)
+
+    def latch(out, m, src, reads, writes):
+        scan(out, m, src, 0.0, A.add, A.max, reads, writes)
+
+    def act(out, in_, func, reads, writes, bias=0.0, scale=1.0, accum=None):
+        op("S", lambda e: e.activation(out, in_, func, bias=bias, scale=scale, accum_out=accum), reads, writes)
+
+    def acopy(out, in_, reads, writes):
+        op("S", lambda e: e.activation(out, in_, F.Copy), reads, writes)
+
+    def quant(name, in_, w, reads):
+        op("V", lambda e: e.quantize_mx(T["Q" + name][:, 0:w], T["Z" + name][:, 0:w], in_), reads, ["Q" + name, "Z" + name])
+
+    def mm(bank, a, a0, b, w, start=True, stop=True):
+        op("P", lambda e: e.matmul_mx(T[bank][:, 0:w], T["Q" + a][:, a0:a0 + 128], T["Z" + a][:, a0:a0 + 128],
+                                      T["Q" + b][:, 0:w], T["Z" + b][:, 0:w], start, stop),
+           ["Q" + a, "Z" + a, "Q" + b, "Z" + b], [bank])
+
+    def iota(name, pattern, base, cm, out=None):
+        if out is None:
+            out = T[name][:]
+        if name in ("vi", "pki", "wi", "v4"):
+            op("G", lambda e: e.iota(out, pattern, base, cm), [], [name])
+        else:
+            op("G", lambda e: e.iota(out, pattern, base, cm, allow_small_or_imprecise_dtypes=True), [], [name])
+
+    def col(k):
+        return T.cols[:, k:k + 1]
+
+    CB, CBH, CBC, CB4, TC, WV, WVB, WVP, J15 = range(9)
+    small = ["cw", "bw", "bw2", "aw", "cw2", "tau", "t1", "kw", "lt", "lf", "k3w", "fa", "fb", "fc", "idx"]
+
+    def sm(name, a=0, b=24):
+        k = 24 * small.index(name)
+        return T.sm[:, k + a:k + b]
+
+    def si(k):
+        return T.si[:, 24 * k:24 * k + 24]
+
+    wrap = slice(15, C, 16)
+
+    dma("Y", "dx", T.wn0[:, 0:4 * C], T.x[:], [], ["T0_%d" % b for b in range(4)])
+    dma("S", "du", T.ut[:], T.u[:], [], ["ut"])
+    dma("Y", "dwc", T.Qlay[:].bitcast(dt.uint8), T.wc[:], ["T0_0"], ["Qlay"])
+    dma("Y", "dws", T.Zlay[:], T.ws[:], [], ["Zlay"])
+    dma("Y", "dv", T.vt[:], T.v[:], [], ["vt"])
+
+    iota("vi", [[1, C]], 128, -1)
+    iota("pki", [[16, 8]], 8, 0, T.pki[:, 0:8])
+    iota("wi", [[16, 8], [0, 64]], 15, -1)
+    iota("cw", [[16, 24]], 15, 0, sm("cw"))
+    iota("v4", [[4, L]], 131, -1)
+    iota("iok", [[1, C]], -64 * 147456, 0)
+
+    op("V", lambda e: e.memset(T.hb[:], 0.0), [], ["hb"])
+    op("V", lambda e: e.memset(sm("cw2", 20, 24), 0.0), [], ["cw2z"])
+    op("V", lambda e: e.memset(T.pw[:, 0:8], 2.0), [], ["two"])
+    ts(T.va[:], T.vi[:], 15, None, A.bitwise_and, None, ["vi"], ["va"])
+    cp(T.pko[:], T.pki[:, 0:8], ["pki"], ["pko"])
+    ts(T.mask[:], T.va[:], 0.0, None, A.is_equal, None, ["va"], ["mask"])
+    ts(col(CB), T.va[:, 15:16], B, None, A.mult, None, ["va"], ["cb"])
+    scan(T.pw[:, 8:15], T.pw[:, 0:7], T.mask[:, 0:7], 0.5, A.mult, A.max, ["two", "mask"], ["pw1"])
+    ts(T.nmask[:], T.va[:], 0.0, None, A.not_equal, None, ["va"], ["nmask"])
+    tt(T.pw[:, 16:23], T.pw[:, 8:15], T.mask[:, 0:7], A.mult, ["pw1", "mask"], ["pw2"])
+    ts(T.wsh[:], T.wi[:], 4, None, A.arith_shift_right, None, ["wi"], ["wsh"])
+    op("V", lambda e: e.tensor_reduce(col(WV), T.pw[:, 16:23], AxisListType.X, A.add), ["pw2"], ["wv"])
+    ts(T.wt[:, 0:512], T.wsh[:], 0.0, -1.0, A.is_equal, A.mult, ["wsh"], ["w1"])
+    ts(col(WVB), col(WV), -147456.0, None, A.mult, None, ["wv"], ["wvb"])
+    ts(col(WVP), col(WV), -3072.0, None, A.mult, None, ["wv"], ["wvp"])
+    act(T.mp[:], T.mask[:], F.Identity, ["mask"], ["mp"], bias=B, scale=-18 * B)
+    act(T.wt[:, 512:1024], T.wt[:, 0:512], F.Identity, ["w1", "wvb"], ["wb"], scale=col(WVB))
+    act(T.wt[:, 1024:1536], T.wt[:, 0:512], F.Identity, ["w1", "wvp"], ["wp"], scale=col(WVP))
+    quant("u", T.ut[:], 128, ["ut"])
+    ts(col(J15), T.va[:, 15:16], 1.0, None, A.mult, None, ["va"], ["j15"])
+    cp(T.Qus[:].bitcast(dt.uint32), T.Qu[:].bitcast(dt.uint32).indirect(T.pko[:]), ["Qu", "pko"], ["Qus"])
+    cp(T.Zus[:], T.Zu[:].indirect(T.pko[:]), ["Zu", "pko"], ["Zus"])
+    ts(col(CBH), T.va[:, 15:16], B, 64 * 3072.0, A.mult, A.add, ["va"], ["cbh"])
+    ts(sm("cw"), sm("cw"), col(J15), None, A.subtract, None, ["cw", "j15"], ["cw"])
+
+    def late_columns():
+        ts(col(CBC), T.va[:, 15:16], BC, None, A.mult, None, ["va"], ["cbc"])
+        ts(T.v4a[:], T.v4[:], 2, 3, A.arith_shift_right, A.bitwise_and, ["v4"], ["v4a"])
+        ts(T.pki[:, 8:9], T.v4[:, 0:1], 3, None, A.bitwise_and, None, ["v4"], ["ti"])
+        ts(T.m4a[:], T.v4a[:], 0.0, -6 * B, A.is_equal, A.mult, ["v4a"], ["m4a"])
+        ts(col(CB4), T.v4a[:, 3:4], B, None, A.mult, None, ["v4a"], ["cb4"])
+        ts(col(TC), T.pki[:, 8:9], -1.0, 3.0, A.mult, A.add, ["ti"], ["tc"])
+
+    def late_tables():
+        iota("iop", [[1, 480]], 0, 0)
+        iota("tab2", [[192, 2 * C]], 0, 0)
+        iota("ones", [[0, 512]], 1, 0)
+        for b in range(4):
+            op("G", lambda e, b=b: e.affine_select(T.et[:, 512 * b:512 * b + 512], T.ones[:], [[-1, 512]], A.is_equal, 0.0, b, 4),
+               ["ones"], ["et%d" % b])
+        iota("c1k", [[0, C]], 1024, 0)
+        for r in range(R):
+            op("G", lambda e, r=r: e.affine_select(T["xt%d" % r][:, C:3 * C], T.tab2[:], [[0, 2 * C]], A.is_gt, EMPTY, -1, 0),
+               ["tab2"], ["tq%d" % r])
+            if r == 0:
+                iota("k3c", [[-511, C]], 0, 0)
+
+    def ranking(nv, row_v, row_s, res_v, res_s, scalar, res_k, early, later):
+        def dest(c):
+            w = WIDTH[c]
+            if c < 8:
+                return T.junk[:, 128 * c:128 * c + 128], "j%d" % c
+            return T["c%d" % (c // 4)][:, c % 4:4 * w:4], "c%d" % c
+
+        def cols_of(u, first):
+            w = WIDTH[4 * u] - 64
+            quant("d%d" % u, T["c%d" % u][:, 0:4 * w], w, ["c%d" % c for c in range(4 * u, 4 * u + 4)])
+            mm("p5", "k", 0, "d%d" % u, w, first, u == 2)
+
+        def sums(c):
+            w = WIDTH[c]
+            k = 192 * (c - 16) + 192
+            t = T["c%d" % (c // 4)]
+            scan(T.sj[:, k - w // 2:k], t[:, c % 4:2 * w:4], t[:, 2 * w + c % 4:4 * w:4], float(-w), A.add, A.add,
+                 ["c%d" % c], ["sj%d" % c])
+
+        def row(c):
+            out, name = dest(c)
+            ts(out, row_v(WIDTH[c]), scalar(c), 2.0, A.is_lt, A.mult, res_k + res_v[0], [name] + res_v[1])
+
+        for c in range(23 - nv, -1, -1):
+            out, name = dest(c)
+            act(out, row_s(WIDTH[c]), F.Sign, res_k + res_s[0], [name, "aw%d" % c] + res_s[1], bias=scalar(c), scale=-1.0,
+                accum=sm("aw", c, c + 1))
+        row(23)
+        for f in early:
+            f()
+        for c in range(22, 19, -1):
+            row(c)
+        todo = list(range(23, 23 - nv, -1))
+        if nv > 4:
+            row(19)
+        else:
+            sums(todo.pop(0))
+        cols_of(5, True)
+        for c in range(18, 23 - nv, -1):
+            row(c)
+        for f in later[:1]:
+            f()
+        sums(todo.pop(0))
+        cols_of(4, False)
+        for f in later[1:2]:
+            f()
+        cols_of(3, False)
+        for f in later[2:]:
+            f()
+        cols_of(2, False)
+        for c in todo:
+            sums(c)
+        k = 192 * (24 - nv - 16) + 191
+        ts(sm("aw", 24 - nv, 24), T.sj[:, k:8 * 192:192], 1.0, None, A.add, None,
+           ["sj%d" % c for c in range(24 - nv, 24)], ["aw%d" % c for c in range(24 - nv, 24)])
+        latch(T.colw[:], T.mp[:, 0:320], T.p5[:, 0:320], ["mp"], ["colw", "p5"])
+        ts(sm("cw2", 0, 16), T.colw[:, 15:256:16], col(CB), 16.0 * nv, A.subtract, A.add, ["colw", "cb"], ["cw2a"])
+        ts(sm("cw2", 16, 20), T.colw[:, 271:320:16], col(CB), 64.0, A.subtract, A.add, ["colw", "cb"], ["cw2b"])
+        tt(sm("tau"), sm("aw"), sm("cw2"), A.add, ["aw%d" % c for c in range(24)] + ["cw2a", "cw2b", "cw2z"], ["tau"])
+
+    for r in range(R):
+        wn, xt, tq = T["wn%d" % r], T["xt%d" % r], "tq%d" % r
+        tn = ["T%d_%d" % (r, b) for b in range(4)]
+        dst, src = T.cores[(rank + STEP[r]) % n], T.cores[(rank - STEP[r]) % n]
+        qt, ql = "t%d" % r, "l%d" % r
+        quant(qt, wn[:, 0:4 * C], C, tn)
+        send(dst, "aq%d" % r, T["Q" + ql][:].bitcast(dt.uint8), T["Q" + qt][:].bitcast(dt.uint8), ["Q" + qt])
+        send(dst, "aq%d" % r, T["Z" + ql][:], T["Z" + qt][:], ["Z" + qt])
+        arrive(src, "aq%d" % r, 2, ["Q" + ql, "Z" + ql])
+        if r == 0:
+            late_tables()
+        mm("p0", "us", 0, qt, C)
+        mm("p2", "u", 0, qt, C)
+        mm("p1", "us", 0, qt, C)
+        if r == 0:
+            quant("k", T.wt[:], 384, ["w1", "wb", "wp"])
+        tt(T.mk[:], T.p0[:, 0:C], T.mask[:], A.mult, ["mask"], ["mk", "p0"])
+        act(T.sg[:], T.p2[:, 0:C], F.Sign, [], ["sg", "p2"])
+        act(T.hb[:, 0:4 * C:4], T.sg[:], F.Relu, ["sg"], ["hb"])
+        scan(T.sw[:], T.nmask[:], T.mk[:], 0.0, A.mult, A.add, ["nmask", "mk"], ["sw"])
+
+        def homes():
+            quant("h", T.hb[:], C, ["hb"])
+            mm("p4", "k", 256, "h", C)
+            mm("p3", "k", 128, "h", C)
+
+        def home_keys():
+            latch(T.hw[:], T.mp[:], T.p4[:, 0:C], ["mp"], ["hw", "p4"])
+            tt(T.brow[:], T.p3[:, 0:C], T.iok[:], A.add, ["iok"], ["brow", "p3"])
+            ts(sm("bw"), T.hw[:, wrap], col(CBH), 48.0, A.subtract, A.mult, ["hw", "cbh"], ["bw"])
+
+        def home_wrap():
+            tt(sm("bw2"), sm("bw"), sm("cw"), A.add, ["bw", "cw"], ["bw2"])
+
+        def packed():
+            tt(T.prow[:], T.p4[:, 0:C], T.iop[:, 0:C], A.add, ["iop"], ["prow", "p4"])
+
+        ranking(NV[0], lambda w: T.p0[:, 0:w], lambda w: T.p1[:, 0:w], ([], ["p0"]), ([], ["p1"]),
+                lambda c: T.sw[:, 16 * c + 15:16 * c + 16], ["sw"], [homes], [home_keys, home_wrap, packed])
+        ts(T.o1[:], sm("tau"), -1.0, 383.0, A.mult, A.add, ["tau"], ["o1"])
+        act(sm("t1"), sm("tau"), F.Identity, ["tau"], ["t1"], bias=192.0 * 383, scale=-192.0)
+        tt(T.krow[:], T.tab2[:].indirect(T.o1[:]), T.brow[:], A.add, ["tab2", "o1", "brow"], ["krow"])
+        tt(sm("kw"), sm("t1"), sm("bw2"), A.add, ["t1", "bw2"], ["kw"])
+        banks = ["p2", "p6", "p7", "p0"]
+
+        def unpack():
+            for b in range(4):
+                mm(banks[b], "e", 128 * b, ql, C)
+
+        def ident():
+            quant("e", T.et[:], 512, ["et%d" % b for b in range(4)])
+
+        if r > 0:
+            unpack()
+        ranking(NV[1], lambda w: T.krow[:, 0:w], lambda w: T.krow[:, 0:w], (["krow"], []), (["krow"], []),
+                lambda c: sm("kw", c, c + 1), ["kw"], [], [late_columns, ident] if r == 0 else [])
+        ts(T.o2[:], sm("tau"), 383.0, 0.5, A.add, A.mult, ["tau"], ["o2"])
+        cp(T.ps[:].indirect(T.o2[:]), T.prow[:], ["prow", "o2"], ["ps"])
+        if r == 0:
+            unpack()
+            act(T.mc[:, 0:C], T.mask[:], F.Identity, ["mask"], ["mca"], bias=BC, scale=-18 * BC)
+            act(T.mc[:, C:2 * C], T.mask[:], F.Identity, ["mask"], ["mcb"], bias=BC, scale=-18 * BC)
+            act(T.m4[:], T.m4a[:], F.Identity, ["m4a"], ["m4"], bias=B)
+        for b in range(4):
+            acopy(T.dw[:, b:4 * C:4], T[banks[b]][:, 0:C], [], ["dw%d" % b, banks[b]])
+        scan(T.qs[:], T.c1k[:], T.ps[:], -4096.0, A.add, A.max, ["c1k", "ps"], ["qs"])
+        latch(T.qw[:], T.mp[:], T.qs[:], ["mp", "qs"], ["qw"])
+        ts(T.oq[:], T.qw[:, wrap], col(CB), 1 / 1024, A.subtract, A.mult, ["qw", "cb"], ["oq"])
+        cp(xt[:, C:3 * C].indirect(T.oq[:]), T.ps[:], ["ps", "oq"], [tq])
+        act(T.tr1[:], xt[:, C:3 * C], F.Identity, [tq], ["tr1"], bias=MAGIC)
+        act(T.tr2[:, 0:C], T.tr1[:, 0:C], F.Identity, ["tr1"], ["tr2a"], bias=-MAGIC / 2, scale=0.5)
+        act(T.tr2[:, C:2 * C], T.tr1[:, C:2 * C], F.Identity, ["tr1"], ["tr2b"], bias=-MAGIC / 2 - 384 * 512, scale=0.5)
+        scan(xt[:, 0:C], xt[:, C:2 * C], T.c1k[:], 383 * EMPTY, A.add, A.max, [tq, "c1k"], ["cum%d" % r])
+        latch(T.xw[:], T.mc[:], xt[:, 0:2 * C], ["mca", "mcb", tq, "cum%d" % r], ["xw"])
+        ts(T.y48[:], T.xw[:, 15:2 * C:16], col(CBC), 1 / EMPTY, A.subtract, A.mult, ["xw", "cbc"], ["y48"])
+        tt(sm("lt"), T.y48[:, 0:24], T.y48[:, 24:48], A.mult, ["y48"], ["lt"])
+        tt(sm("lf"), sm("lt"), sm("cw"), A.max, ["lt", "cw"], ["lf"])
+        ts(T.ol[:], sm("lf"), 0.25, None, A.add, None, ["lf"], ["ol"])
+        tt(T.k3[:], T.tr2[:].indirect(T.ol[:]), T.k3c[:], A.add, ["tr2a", "tr2b", "ol", "k3c"], ["k3"])
+        acopy(T.grow[:], xt[:, C:3 * C].indirect(T.ol[:]), [tq, "ol"], ["grow"])
+        latch(T.k3s[:], T.mp[:], T.k3[:], ["mp", "k3"], ["k3s"])
+        ts(sm("k3w"), T.k3s[:, wrap], col(CB), None, A.subtract, None, ["k3s", "cb"], ["k3w"])
+        ranking(NV[2], lambda w: T.k3[:, 0:w], lambda w: T.k3[:, 0:w], (["k3"], []), (["k3"], []),
+                lambda c: sm("k3w", c, c + 1), ["k3w"], [], [])
+        ts(T.o3[:], sm("tau"), 383.0, 0.5, A.add, A.mult, ["tau"], ["o3"])
+        cp(T.bl[:].indirect(T.o3[:]), T.grow[:], ["grow", "o3"], ["bl"])
+        latch(T.b4[:], T.m4[:], T.bl[:, 0:L], ["m4", "bl"], ["b4"])
+        ts(si(0), T.b4[:, 3:L:4], col(CB4), None, A.subtract, None, ["b4", "cb4"], ["bi"])
+        ts(si(1), si(0), 1023, None, A.bitwise_and, None, ["bi"], ["bj"])
+        ob, oa = T["ob%d" % r], T["oa%d" % r]
+        ts(ob[:], si(1), 4.0, col(TC), A.mult, A.add, ["bj", "tc"], ["ob%d" % r])
+        send(dst, "ao%d" % r, oa[:], ob[:], ["ob%d" % r])
+        arrive(src, "ao%d" % r, 1, ["oa%d" % r])
+        latch(T.gw[:], T.mp[:], T.grow[:], ["mp", "grow"], ["gw"])
+        ts(sm("fa"), sm("tau"), -191.0, None, A.is_lt, None, ["tau"], ["fa"])
+        ts(sm("fb"), sm("tau"), 1151.0, 0.5, A.add, A.mult, ["tau"], ["fb"])
+        ts(si(2), T.gw[:, wrap], col(CB), None, A.subtract, None, ["gw", "cb"], ["mi"])
+        tt(sm("fc"), sm("fa"), sm("fb"), A.mult, ["fa", "fb"], ["fc"])
+        ts(si(3), si(2), 1023, None, A.bitwise_and, None, ["mi"], ["mj"])
+        tt(sm("idx"), si(3), sm("fc"), A.max, ["mj", "fc"], ["idx"])
+        for t in range(4):
+            ts(T.ov[:, 24 * t:24 * t + 24], sm("idx"), 4.0, float(t), A.mult, A.add, ["idx"], ["ov%d" % t])
+        if r == R - 1:
+            cp(T.oo[:], sm("idx"), ["idx"], ["oo"])
+            acopy(T.otr[:], T.iop[:].indirect(T.oo[:]), ["iop", "oo"], ["otr"])
+            for k in range(8):
+                dma("Y", "dot", T.ot[k:k + 1, :], T.otr[16 * k:16 * k + 1, :], ["otr"], [])
+            quant("v", T.vt[:], 128, ["vt"])
+        dws = ["dw%d" % b for b in range(4)]
+        cp(wn[:, 4 * C:4 * C + 192], T.dw[:].indirect(oa[:, 0:12]), dws + ["oa%d" % r], ["Ba%d" % r])
+        acopy(wn[:, 4 * C + 192:4 * C + 384], T.dw[:].indirect(oa[:, 12:24]), dws + ["oa%d" % r], ["Bb%d" % r])
+        win = tn + ["Ba%d" % r, "Bb%d" % r]
+        for t in range(4):
+            (cp if t < 2 else acopy)(T.vv[:, t:4 * C:4], wn[:].indirect(T.ov[:, 24 * t:24 * t + 24]), win + ["ov%d" % t], ["vv%d" % t])
+        quant("m", T.vv[:], C, ["vv%d" % t for t in range(4)])
+        rb = ["p0", "p1", "p3", "p4"]
+        for b in range(4):
+            mm(rb[b], "lay", 128 * b, "m", C)
+        for b in (0, 1):
+            ts(T.v64[:, C * b:C * b + C], T.vv[:, b:4 * C:4], 64.0, None, A.mult, None, ["vv%d" % b], ["v64%d" % b])
+        for b in (2, 3):
+            act(T.v64[:, C * b:C * b + C], T.vv[:, b:4 * C:4], F.Identity, ["vv%d" % b], ["v64%d" % b], scale=64.0)
+        new = T["wn%d" % (r + 1)] if r + 1 < R else T.tf
+        for b in range(4):
+            tt(T.tmp[:, C * b:C * b + C], T[rb[b]][:, 0:C], T.v64[:, C * b:C * b + C], A.add, ["v64%d" % b], ["tmp%d" % b, rb[b]])
+            act(new[:, b:4 * C:4], T.tmp[:, C * b:C * b + C], F.Identity, ["tmp%d" % b], ["T%d_%d" % (r + 1, b)], scale=0.015625)
+
+    quant("f", T.tf[:], C, ["T%d_%d" % (R, b) for b in range(4)])
+    mm("p2", "v", 0, "f", C)
+    dma("Y", "doa", T.oc[:], T.Qf[:].bitcast(dt.uint8), ["Qf"], [])
+    for k in range(4):
+        dma("S" if k < 2 else "Y", "dob" if k < 2 else "doa", T.osc[4 * k:4 * k + 4, :], T.Zf[32 * k:32 * k + 4, :], ["Zf"], [])
+    cp(T.yo[:], T.p2[:, 0:C], [], ["yo", "p2"])
+    dma("S", "dob", T.y[:], T.yo[:], ["yo"], [])
+    _emit(g, T, ops)

@@ -3,12 +3,14 @@ from concourse.mybir import dt, AluOpType, AxisListType, ActivationFunctionType
 A = AluOpType
 F = ActivationFunctionType
 C, L, R = 384, 96, 3
+H = C // 2
 STEP = [1, 2, 4]
 X4 = "float8_e4m3fn_x4"
 B = float(2 ** 20)
 BC = float(2 ** 42)
 EMPTY = float(2 ** 32)
 MAGIC = 1.5 * 2 ** 33
+TINY = 2.0 ** -120
 NV = [4, 6, 6]
 WIDTH = [128] * 8 + [192] * 4 + [256] * 4 + [320] * 4 + [384] * 4
 
@@ -19,16 +21,16 @@ def _sb(name, n, dtype):
     SCRATCH[name] = ("sbuf", [128, n], dtype)
 
 
-for _n, _w in dict(mask=C, nmask=C, mp=C, mc=2 * C, m4=L, m4a=L, cols=16, pw=32, iok=C, iop=480, k3c=C, tab2=2 * C,
+for _n, _w in dict(mask=C, nmask=C, mp=C, mc=C, m4=L, m4a=L, cols=16, pw=32, iok=C, iop=480, k3c=C, tab2=2 * C,
                    c1k=C, mk=C, sw=C, brow=C, prow=C, hw=C, sm=24 * 16, colw=320, krow=C,
-                   ps=C, qs=C, qw=C, xw=2 * C, y48=48, tr1=2 * C, tr2=2 * C, grow=C, k3=C, k3s=C,
+                   ps=C, qs=C, qw=C, xw=2 * C, y48=48, tr1=2 * C, tr2=2 * C, grow=C, k3=C, k3s=C, k3r=C,
                    bl=C, b4=L, gw=C, tmp=4 * C, yo=C, otr=C).items():
     _sb(_n, _w, "float32")
 for _n, _w in dict(vi=C, va=C, pki=16, wi=512, wsh=512, v4=L, v4a=L, si=24 * 4).items():
     _sb(_n, _w, "int32")
 for _n, _w in dict(pko=8, o1=24, o2=24, oq=24, ol=24, o3=24, ov=96, oo=24).items():
     _sb(_n, _w, "uint16")
-for _n, _w in dict(ut=512, vt=512, wt=1536, ones=512, et=2048, sg=C, hb=4 * C, junk=1024, sj=8 * 192, dw=4 * C, vv=4 * C,
+for _n, _w in dict(ut=512, vt=512, wt=1536, ones=512, et=2048, hb=4 * C, junk=1024, sj=8 * 192, dw=4 * C, vv=4 * C,
                    v64=4 * C, tf=4 * C, c2=768, c3=1024, c4=1280, c5=1536).items():
     _sb(_n, _w, "bfloat16")
 for _n, _w in dict(u=128, us=128, v=128, lay=512, k=384, e=512, h=C, m=C, f=C, d2=128, d3=192, d4=256, d5=320).items():
@@ -145,7 +147,16 @@ def rank_program(g, core, T, topo):
     def mm(bank, a, a0, b, w, start=True, stop=True):
         op("P", lambda e: e.matmul_mx(T[bank][:, 0:w], T["Q" + a][:, a0:a0 + 128], T["Z" + a][:, a0:a0 + 128],
                                       T["Q" + b][:, 0:w], T["Z" + b][:, 0:w], start, stop),
-           ["Q" + a, "Z" + a, "Q" + b, "Z" + b], [bank])
+           ["Q" + a, "Z" + a, "Q" + b, "Z" + b, b + "0", b + "1"], [bank])
+
+    def quant_halves(name, tile, state):
+        for h in range(2):
+            op("V", lambda e, h=h: e.quantize_mx(T["Q" + name][:, H * h:H * h + H], T["Z" + name][:, H * h:H * h + H],
+                                                 tile[:, 4 * H * h:4 * H * h + 4 * H]), state[:3] + [state[3 + h]], [name + str(h)])
+
+    def mm_half(bank, a, b, h):
+        op("P", lambda e: e.matmul_mx(T[bank][:, 0:H], T["Q" + a][:], T["Z" + a][:], T["Q" + b][:, H * h:H * h + H],
+                                      T["Z" + b][:, H * h:H * h + H], True, True), ["Q" + a, "Z" + a, b + str(h)], [bank])
 
     def iota(name, pattern, base, cm, out=None):
         if out is None:
@@ -158,8 +169,11 @@ def rank_program(g, core, T, topo):
     def col(k):
         return T.cols[:, k:k + 1]
 
+    def state(r):
+        return ["T%d_%s" % (r, b) for b in ("0", "1", "2", "30", "31")]
+
     CB, CBH, CBC, CB4, TC, WV, WVB, WVP, J15 = range(9)
-    small = ["cw", "bw", "bw2", "aw", "cw2", "tau", "t1", "kw", "lt", "lf", "k3w", "fa", "fb", "fc", "idx"]
+    small = ["cw", "bw", "bw2", "aw", "cw2", "tau", "t1", "kw", "lt", "lf", "fa", "fb", "fc", "idx"]
 
     def sm(name, a=0, b=24):
         k = 24 * small.index(name)
@@ -170,7 +184,7 @@ def rank_program(g, core, T, topo):
 
     wrap = slice(15, C, 16)
 
-    dma("Y", "dx", T.wn0[:, 0:4 * C], T.x[:], [], ["T0_%d" % b for b in range(4)])
+    dma("Y", "dx", T.wn0[:, 0:4 * C], T.x[:], [], state(0))
     dma("S", "du", T.ut[:], T.u[:], [], ["ut"])
     dma("Y", "dwc", T.Qlay[:].bitcast(dt.uint8), T.wc[:], ["T0_0"], ["Qlay"])
     dma("Y", "dws", T.Zlay[:], T.ws[:], [], ["Zlay"])
@@ -181,7 +195,7 @@ def rank_program(g, core, T, topo):
     iota("wi", [[16, 8], [0, 64]], 15, -1)
     iota("cw", [[16, 24]], 15, 0, sm("cw"))
     iota("v4", [[4, L]], 131, -1)
-    iota("iok", [[1, C]], -64 * 147456, 0)
+    iota("iok", [[1, C]], 127 * 1536, 0)
 
     op("V", lambda e: e.memset(T.hb[:], 0.0), [], ["hb"])
     op("V", lambda e: e.memset(sm("cw2", 20, 24), 0.0), [], ["cw2z"])
@@ -189,35 +203,38 @@ def rank_program(g, core, T, topo):
     ts(T.va[:], T.vi[:], 15, None, A.bitwise_and, None, ["vi"], ["va"])
     cp(T.pko[:], T.pki[:, 0:8], ["pki"], ["pko"])
     ts(T.mask[:], T.va[:], 0.0, None, A.is_equal, None, ["va"], ["mask"])
-    ts(col(CB), T.va[:, 15:16], B, None, A.mult, None, ["va"], ["cb"])
-    scan(T.pw[:, 8:15], T.pw[:, 0:7], T.mask[:, 0:7], 0.5, A.mult, A.max, ["two", "mask"], ["pw1"])
-    ts(T.nmask[:], T.va[:], 0.0, None, A.not_equal, None, ["va"], ["nmask"])
-    tt(T.pw[:, 16:23], T.pw[:, 8:15], T.mask[:, 0:7], A.mult, ["pw1", "mask"], ["pw2"])
     ts(T.wsh[:], T.wi[:], 4, None, A.arith_shift_right, None, ["wi"], ["wsh"])
-    op("V", lambda e: e.tensor_reduce(col(WV), T.pw[:, 16:23], AxisListType.X, A.add), ["pw2"], ["wv"])
+    scan(T.pw[:, 8:15], T.pw[:, 0:7], T.mask[:, 0:7], 0.5, A.mult, A.max, ["two", "mask"], ["pw1"])
     ts(T.wt[:, 0:512], T.wsh[:], 0.0, -1.0, A.is_equal, A.mult, ["wsh"], ["w1"])
-    ts(col(WVB), col(WV), -147456.0, None, A.mult, None, ["wv"], ["wvb"])
-    ts(col(WVP), col(WV), -3072.0, None, A.mult, None, ["wv"], ["wvp"])
-    act(T.mp[:], T.mask[:], F.Identity, ["mask"], ["mp"], bias=B, scale=-18 * B)
-    act(T.wt[:, 512:1024], T.wt[:, 0:512], F.Identity, ["w1", "wvb"], ["wb"], scale=col(WVB))
-    act(T.wt[:, 1024:1536], T.wt[:, 0:512], F.Identity, ["w1", "wvp"], ["wp"], scale=col(WVP))
+    tt(T.pw[:, 16:23], T.pw[:, 8:15], T.mask[:, 0:7], A.mult, ["pw1", "mask"], ["pw2"])
     quant("u", T.ut[:], 128, ["ut"])
-    ts(col(J15), T.va[:, 15:16], 1.0, None, A.mult, None, ["va"], ["j15"])
+    op("V", lambda e: e.tensor_reduce(col(WV), T.pw[:, 16:23], AxisListType.X, A.add), ["pw2"], ["wv"])
     cp(T.Qus[:].bitcast(dt.uint32), T.Qu[:].bitcast(dt.uint32).indirect(T.pko[:]), ["Qu", "pko"], ["Qus"])
     cp(T.Zus[:], T.Zu[:].indirect(T.pko[:]), ["Zu", "pko"], ["Zus"])
-    ts(col(CBH), T.va[:, 15:16], B, 64 * 3072.0, A.mult, A.add, ["va"], ["cbh"])
-    ts(sm("cw"), sm("cw"), col(J15), None, A.subtract, None, ["cw", "j15"], ["cw"])
+    act(T.nmask[:], T.mask[:], F.Identity, ["mask"], ["nmask"], bias=1.0, scale=-1.0)
+    act(T.mp[:], T.mask[:], F.Identity, ["mask"], ["mp"], bias=B, scale=-18 * B)
+    act(col(WVB), col(WV), F.Identity, ["wv"], ["wvb"], scale=-73728.0)
+    act(col(WVP), col(WV), F.Identity, ["wv"], ["wvp"], scale=-1536.0)
+    act(T.wt[:, 512:1024], T.wt[:, 0:512], F.Identity, ["w1", "wvb"], ["wb"], scale=col(WVB))
+    act(T.wt[:, 1024:1536], T.wt[:, 0:512], F.Identity, ["w1", "wvp"], ["wp"], scale=col(WVP))
+
+    def columns():
+        ts(col(J15), T.va[:, 15:16], 1.0, None, A.mult, None, ["va"], ["j15"])
+        ts(col(CB), T.va[:, 15:16], B, None, A.mult, None, ["va"], ["cb"])
+        ts(col(CBH), T.va[:, 15:16], B, -4064.0, A.mult, A.add, ["va"], ["cbh"])
+        ts(col(CBC), T.va[:, 15:16], BC, None, A.mult, None, ["va"], ["cbc"])
+        ts(sm("cw"), sm("cw"), col(J15), None, A.subtract, None, ["cw", "j15"], ["cw"])
 
     def late_columns():
-        ts(col(CBC), T.va[:, 15:16], BC, None, A.mult, None, ["va"], ["cbc"])
         ts(T.v4a[:], T.v4[:], 2, 3, A.arith_shift_right, A.bitwise_and, ["v4"], ["v4a"])
         ts(T.pki[:, 8:9], T.v4[:, 0:1], 3, None, A.bitwise_and, None, ["v4"], ["ti"])
+
+    def last_columns():
         ts(T.m4a[:], T.v4a[:], 0.0, -6 * B, A.is_equal, A.mult, ["v4a"], ["m4a"])
         ts(col(CB4), T.v4a[:, 3:4], B, None, A.mult, None, ["v4a"], ["cb4"])
         ts(col(TC), T.pki[:, 8:9], -1.0, 3.0, A.mult, A.add, ["ti"], ["tc"])
 
     def late_tables():
-        iota("iop", [[1, 480]], 0, 0)
         iota("tab2", [[192, 2 * C]], 0, 0)
         iota("ones", [[0, 512]], 1, 0)
         for b in range(4):
@@ -229,6 +246,7 @@ def rank_program(g, core, T, topo):
                ["tab2"], ["tq%d" % r])
             if r == 0:
                 iota("k3c", [[-511, C]], 0, 0)
+        iota("iop", [[1, 480]], 0, 0)
 
     def ranking(nv, row_v, row_s, res_v, res_s, scalar, res_k, early, later):
         def dest(c):
@@ -260,19 +278,21 @@ def rank_program(g, core, T, topo):
         row(23)
         for f in early:
             f()
-        for c in range(22, 19, -1):
+        for c in range(22, max(19, 23 - nv), -1):
             row(c)
         todo = list(range(23, 23 - nv, -1))
         if nv > 4:
             row(19)
-        else:
+            cols_of(5, True)
+            for c in range(18, 23 - nv, -1):
+                row(c)
+            for f in later[:1]:
+                f()
             sums(todo.pop(0))
-        cols_of(5, True)
-        for c in range(18, 23 - nv, -1):
-            row(c)
-        for f in later[:1]:
-            f()
-        sums(todo.pop(0))
+        else:
+            for f in later[:1]:
+                f()
+            cols_of(5, True)
         cols_of(4, False)
         for f in later[1:2]:
             f()
@@ -280,38 +300,51 @@ def rank_program(g, core, T, topo):
         for f in later[2:]:
             f()
         cols_of(2, False)
-        for c in todo:
+        for c in todo[:3]:
             sums(c)
         k = 192 * (24 - nv - 16) + 191
-        ts(sm("aw", 24 - nv, 24), T.sj[:, k:8 * 192:192], 1.0, None, A.add, None,
-           ["sj%d" % c for c in range(24 - nv, 24)], ["aw%d" % c for c in range(24 - nv, 24)])
+
+        def own():
+            ts(sm("aw", 24 - nv, 24), T.sj[:, k:8 * 192:192], 1.0, None, A.add, None,
+               ["sj%d" % c for c in range(24 - nv, 24)], ["aw%d" % c for c in range(24 - nv, 24)])
+
         latch(T.colw[:], T.mp[:, 0:320], T.p5[:, 0:320], ["mp"], ["colw", "p5"])
+        for c in todo[3:]:
+            sums(c)
+        if not todo[3:]:
+            own()
         ts(sm("cw2", 0, 16), T.colw[:, 15:256:16], col(CB), 16.0 * nv, A.subtract, A.add, ["colw", "cb"], ["cw2a"])
-        ts(sm("cw2", 16, 20), T.colw[:, 271:320:16], col(CB), 64.0, A.subtract, A.add, ["colw", "cb"], ["cw2b"])
+        ts(sm("cw2", 16, 20), T.colw[:, 271:320:16], col(CB), 16.0 * min(nv, 4), A.subtract, A.add, ["colw", "cb"], ["cw2b"])
+        if todo[3:]:
+            own()
         tt(sm("tau"), sm("aw"), sm("cw2"), A.add, ["aw%d" % c for c in range(24)] + ["cw2a", "cw2b", "cw2z"], ["tau"])
 
     for r in range(R):
         wn, xt, tq = T["wn%d" % r], T["xt%d" % r], "tq%d" % r
-        tn = ["T%d_%d" % (r, b) for b in range(4)]
+        tn = state(r)
         dst, src = T.cores[(rank + STEP[r]) % n], T.cores[(rank - STEP[r]) % n]
         qt, ql = "t%d" % r, "l%d" % r
-        quant(qt, wn[:, 0:4 * C], C, tn)
-        send(dst, "aq%d" % r, T["Q" + ql][:].bitcast(dt.uint8), T["Q" + qt][:].bitcast(dt.uint8), ["Q" + qt])
-        send(dst, "aq%d" % r, T["Z" + ql][:], T["Z" + qt][:], ["Z" + qt])
+        quant_halves(qt, wn, tn)
+        send(dst, "aq%d" % r, T["Q" + ql][:].bitcast(dt.uint8), T["Q" + qt][:].bitcast(dt.uint8), [qt + "0", qt + "1"])
+        send(dst, "aq%d" % r, T["Z" + ql][:], T["Z" + qt][:], [qt + "0", qt + "1"])
         arrive(src, "aq%d" % r, 2, ["Q" + ql, "Z" + ql])
         if r == 0:
             late_tables()
-        mm("p0", "us", 0, qt, C)
+        mm_half("p6", "us", qt, 0)
+        mm_half("p7", "us", qt, 1)
         mm("p2", "u", 0, qt, C)
+        mm("p0", "us", 0, qt, C)
         mm("p1", "us", 0, qt, C)
         if r == 0:
-            quant("k", T.wt[:], 384, ["w1", "wb", "wp"])
-        tt(T.mk[:], T.p0[:, 0:C], T.mask[:], A.mult, ["mask"], ["mk", "p0"])
-        act(T.sg[:], T.p2[:, 0:C], F.Sign, [], ["sg", "p2"])
-        act(T.hb[:, 0:4 * C:4], T.sg[:], F.Relu, ["sg"], ["hb"])
-        scan(T.sw[:], T.nmask[:], T.mk[:], 0.0, A.mult, A.add, ["nmask", "mk"], ["sw"])
+            columns()
+        tt(T.mk[:, 0:H], T.p6[:, 0:H], T.mask[:, 0:H], A.mult, ["mask"], ["mka", "p6"])
+        tt(T.mk[:, H:C], T.p7[:, 0:H], T.mask[:, 0:H], A.mult, ["mask"], ["mkb", "p7"])
+        act(T.hb[:, 0:4 * C:4], T.p2[:, 0:C], F.Sign, [], ["hb", "p2"], bias=-TINY)
+        scan(T.sw[:], T.nmask[:], T.mk[:], 0.0, A.mult, A.add, ["nmask", "mka", "mkb"], ["sw"])
 
         def homes():
+            if r == 0:
+                quant("k", T.wt[:], 384, ["w1", "wb", "wp"])
             quant("h", T.hb[:], C, ["hb"])
             mm("p4", "k", 256, "h", C)
             mm("p3", "k", 128, "h", C)
@@ -325,10 +358,10 @@ def rank_program(g, core, T, topo):
             tt(sm("bw2"), sm("bw"), sm("cw"), A.add, ["bw", "cw"], ["bw2"])
 
         def packed():
-            tt(T.prow[:], T.p4[:, 0:C], T.iop[:, 0:C], A.add, ["iop"], ["prow", "p4"])
+            tt(T.prow[:], T.p4[:, 0:C], T.iok[:], A.add, ["iok"], ["prow", "p4"])
 
         ranking(NV[0], lambda w: T.p0[:, 0:w], lambda w: T.p1[:, 0:w], ([], ["p0"]), ([], ["p1"]),
-                lambda c: T.sw[:, 16 * c + 15:16 * c + 16], ["sw"], [homes], [home_keys, home_wrap, packed])
+                lambda c: T.sw[:, 16 * c + 15:16 * c + 16], ["sw"], [homes], [home_keys, packed, home_wrap])
         ts(T.o1[:], sm("tau"), -1.0, 383.0, A.mult, A.add, ["tau"], ["o1"])
         act(sm("t1"), sm("tau"), F.Identity, ["tau"], ["t1"], bias=192.0 * 383, scale=-192.0)
         tt(T.krow[:], T.tab2[:].indirect(T.o1[:]), T.brow[:], A.add, ["tab2", "o1", "brow"], ["krow"])
@@ -345,13 +378,12 @@ def rank_program(g, core, T, topo):
         if r > 0:
             unpack()
         ranking(NV[1], lambda w: T.krow[:, 0:w], lambda w: T.krow[:, 0:w], (["krow"], []), (["krow"], []),
-                lambda c: sm("kw", c, c + 1), ["kw"], [], [late_columns, ident] if r == 0 else [])
+                lambda c: sm("kw", c, c + 1), ["kw"], [], [late_columns, last_columns, ident] if r == 0 else [])
         ts(T.o2[:], sm("tau"), 383.0, 0.5, A.add, A.mult, ["tau"], ["o2"])
         cp(T.ps[:].indirect(T.o2[:]), T.prow[:], ["prow", "o2"], ["ps"])
         if r == 0:
             unpack()
-            act(T.mc[:, 0:C], T.mask[:], F.Identity, ["mask"], ["mca"], bias=BC, scale=-18 * BC)
-            act(T.mc[:, C:2 * C], T.mask[:], F.Identity, ["mask"], ["mcb"], bias=BC, scale=-18 * BC)
+            act(T.mc[:], T.mask[:], F.Identity, ["mask"], ["mc"], bias=BC, scale=-18 * BC)
             act(T.m4[:], T.m4a[:], F.Identity, ["m4a"], ["m4"], bias=B)
         for b in range(4):
             acopy(T.dw[:, b:4 * C:4], T[banks[b]][:, 0:C], [], ["dw%d" % b, banks[b]])
@@ -363,19 +395,22 @@ def rank_program(g, core, T, topo):
         act(T.tr2[:, 0:C], T.tr1[:, 0:C], F.Identity, ["tr1"], ["tr2a"], bias=-MAGIC / 2, scale=0.5)
         act(T.tr2[:, C:2 * C], T.tr1[:, C:2 * C], F.Identity, ["tr1"], ["tr2b"], bias=-MAGIC / 2 - 384 * 512, scale=0.5)
         scan(xt[:, 0:C], xt[:, C:2 * C], T.c1k[:], 383 * EMPTY, A.add, A.max, [tq, "c1k"], ["cum%d" % r])
-        latch(T.xw[:], T.mc[:], xt[:, 0:2 * C], ["mca", "mcb", tq, "cum%d" % r], ["xw"])
-        ts(T.y48[:], T.xw[:, 15:2 * C:16], col(CBC), 1 / EMPTY, A.subtract, A.mult, ["xw", "cbc"], ["y48"])
+        latch(T.xw[:, C:2 * C], T.mc[:], xt[:, C:2 * C], ["mc", tq], ["xwb"])
+        latch(T.xw[:, 0:C], T.mc[:], xt[:, 0:C], ["mc", "cum%d" % r], ["xwa"])
+        ts(T.y48[:], T.xw[:, 15:2 * C:16], col(CBC), 1 / EMPTY, A.subtract, A.mult, ["xwa", "xwb", "cbc"], ["y48"])
         tt(sm("lt"), T.y48[:, 0:24], T.y48[:, 24:48], A.mult, ["y48"], ["lt"])
         tt(sm("lf"), sm("lt"), sm("cw"), A.max, ["lt", "cw"], ["lf"])
         ts(T.ol[:], sm("lf"), 0.25, None, A.add, None, ["lf"], ["ol"])
         tt(T.k3[:], T.tr2[:].indirect(T.ol[:]), T.k3c[:], A.add, ["tr2a", "tr2b", "ol", "k3c"], ["k3"])
         acopy(T.grow[:], xt[:, C:3 * C].indirect(T.ol[:]), [tq, "ol"], ["grow"])
         latch(T.k3s[:], T.mp[:], T.k3[:], ["mp", "k3"], ["k3s"])
-        ts(sm("k3w"), T.k3s[:, wrap], col(CB), None, A.subtract, None, ["k3s", "cb"], ["k3w"])
-        ranking(NV[2], lambda w: T.k3[:, 0:w], lambda w: T.k3[:, 0:w], (["k3"], []), (["k3"], []),
-                lambda c: sm("k3w", c, c + 1), ["k3w"], [], [])
+        act(T.k3r[:], T.k3[:], F.Identity, ["k3", "cb"], ["k3r"], bias=col(CB))
+        ranking(NV[2], lambda w: T.k3r[:, 0:w], lambda w: T.k3r[:, 0:w], (["k3r"], []), (["k3r"], []),
+                lambda c: T.k3s[:, 16 * c + 15:16 * c + 16], ["k3s"], [], [])
         ts(T.o3[:], sm("tau"), 383.0, 0.5, A.add, A.mult, ["tau"], ["o3"])
+        ts(sm("fa"), sm("tau"), -191.0, None, A.is_lt, None, ["tau"], ["fa"])
         cp(T.bl[:].indirect(T.o3[:]), T.grow[:], ["grow", "o3"], ["bl"])
+        ts(sm("fb"), sm("tau"), 1151.0, 0.5, A.add, A.mult, ["tau"], ["fb"])
         latch(T.b4[:], T.m4[:], T.bl[:, 0:L], ["m4", "bl"], ["b4"])
         ts(si(0), T.b4[:, 3:L:4], col(CB4), None, A.subtract, None, ["b4", "cb4"], ["bi"])
         ts(si(1), si(0), 1023, None, A.bitwise_and, None, ["bi"], ["bj"])
@@ -384,10 +419,8 @@ def rank_program(g, core, T, topo):
         send(dst, "ao%d" % r, oa[:], ob[:], ["ob%d" % r])
         arrive(src, "ao%d" % r, 1, ["oa%d" % r])
         latch(T.gw[:], T.mp[:], T.grow[:], ["mp", "grow"], ["gw"])
-        ts(sm("fa"), sm("tau"), -191.0, None, A.is_lt, None, ["tau"], ["fa"])
-        ts(sm("fb"), sm("tau"), 1151.0, 0.5, A.add, A.mult, ["tau"], ["fb"])
-        ts(si(2), T.gw[:, wrap], col(CB), None, A.subtract, None, ["gw", "cb"], ["mi"])
         tt(sm("fc"), sm("fa"), sm("fb"), A.mult, ["fa", "fb"], ["fc"])
+        ts(si(2), T.gw[:, wrap], col(CB), None, A.subtract, None, ["gw", "cb"], ["mi"])
         ts(si(3), si(2), 1023, None, A.bitwise_and, None, ["mi"], ["mj"])
         tt(sm("idx"), si(3), sm("fc"), A.max, ["mj", "fc"], ["idx"])
         for t in range(4):
@@ -406,22 +439,27 @@ def rank_program(g, core, T, topo):
             (cp if t < 2 else acopy)(T.vv[:, t:4 * C:4], wn[:].indirect(T.ov[:, 24 * t:24 * t + 24]), win + ["ov%d" % t], ["vv%d" % t])
         quant("m", T.vv[:], C, ["vv%d" % t for t in range(4)])
         rb = ["p0", "p1", "p3", "p4"]
-        for b in range(4):
+        for b in (0, 3, 1, 2):
             mm(rb[b], "lay", 128 * b, "m", C)
-        for b in (0, 1):
-            ts(T.v64[:, C * b:C * b + C], T.vv[:, b:4 * C:4], 64.0, None, A.mult, None, ["vv%d" % b], ["v64%d" % b])
-        for b in (2, 3):
+        ts(T.v64[:, 0:C], T.vv[:, 0:4 * C:4], 64.0, None, A.mult, None, ["vv0"], ["v640"])
+        for b in (2, 1):
             act(T.v64[:, C * b:C * b + C], T.vv[:, b:4 * C:4], F.Identity, ["vv%d" % b], ["v64%d" % b], scale=64.0)
+        act(T.tmp[:, 3 * C:4 * C], T.p4[:, 0:C], F.Identity, [], ["tmp3", "p4"], scale=0.015625)
         new = T["wn%d" % (r + 1)] if r + 1 < R else T.tf
-        for b in range(4):
+        for b in range(3):
             tt(T.tmp[:, C * b:C * b + C], T[rb[b]][:, 0:C], T.v64[:, C * b:C * b + C], A.add, ["v64%d" % b], ["tmp%d" % b, rb[b]])
             act(new[:, b:4 * C:4], T.tmp[:, C * b:C * b + C], F.Identity, ["tmp%d" % b], ["T%d_%d" % (r + 1, b)], scale=0.015625)
+        for h in range(2):
+            tt(new[:, 4 * H * h + 3:4 * H * h + 4 * H:4], T.tmp[:, 3 * C + H * h:3 * C + H * h + H],
+               T.vv[:, 4 * H * h + 3:4 * H * h + 4 * H:4], A.add, ["tmp3", "vv3"], ["T%d_3%d" % (r + 1, h)])
 
-    quant("f", T.tf[:], C, ["T%d_%d" % (R, b) for b in range(4)])
-    mm("p2", "v", 0, "f", C)
-    dma("Y", "doa", T.oc[:], T.Qf[:].bitcast(dt.uint8), ["Qf"], [])
+    quant_halves("f", T.tf, state(R))
+    mm_half("p6", "v", "f", 0)
+    mm_half("p7", "v", "f", 1)
+    dma("Y", "doa", T.oc[:], T.Qf[:].bitcast(dt.uint8), ["f0", "f1"], [])
+    cp(T.yo[:, 0:H], T.p6[:, 0:H], [], ["ya", "p6"])
+    cp(T.yo[:, H:C], T.p7[:, 0:H], [], ["yb", "p7"])
     for k in range(4):
-        dma("S" if k < 2 else "Y", "dob" if k < 2 else "doa", T.osc[4 * k:4 * k + 4, :], T.Zf[32 * k:32 * k + 4, :], ["Zf"], [])
-    cp(T.yo[:], T.p2[:, 0:C], [], ["yo", "p2"])
-    dma("S", "dob", T.y[:], T.yo[:], ["yo"], [])
+        dma("S" if k < 2 else "Y", "dob" if k < 2 else "doa", T.osc[4 * k:4 * k + 4, :], T.Zf[32 * k:32 * k + 4, :], ["f0", "f1"], [])
+    dma("S", "dob", T.y[:], T.yo[:], ["ya", "yb"], [])
     _emit(g, T, ops)

@@ -21,16 +21,16 @@ def _sb(name, n, dtype):
     SCRATCH[name] = ("sbuf", [128, n], dtype)
 
 
-for _n, _w in dict(mask=C, nmask=C, mp=C, mc=C, m4=L, m4a=L, cols=16, pw=32, iok=C, iop=480, k3c=C, tab2=2 * C,
-                   c1k=C, mk=C, sw=C, brow=C, prow=C, hw=C, sm=24 * 16, colw=320, krow=C,
-                   ps=C, qs=C, qw=C, xw=2 * C, y48=48, tr1=2 * C, tr2=2 * C, grow=C, k3=C, k3s=C, k3r=C,
+for _n, _w in dict(mask=H, nmask=H, mp=C, mc=C, m4=2 * L, cols=16, pw=32, iok=C, iob=C, iop=2 * C, k3c=C,
+                   c1k=C, mk=C, sw=C, brow=C, prow=C, hw=C, sm=24 * 18, colw=320, krow=C,
+                   ps=C, qs=C, qw=C, xw=2 * C, tr1=2 * C, tr2=2 * C, grow=C, k3=C, k3s=C, k3r=C,
                    bl=C, b4=L, gw=C, tmp=4 * C, yo=C, otr=C).items():
     _sb(_n, _w, "float32")
-for _n, _w in dict(vi=C, va=C, pki=16, wi=512, wsh=512, v4=L, v4a=L, si=24 * 4).items():
+for _n, _w in dict(vi=H, va=H, pki=16, wi=128, wsh=128, v4=L, v4a=L, si=24 * 4).items():
     _sb(_n, _w, "int32")
 for _n, _w in dict(pko=8, o1=24, o2=24, oq=24, ol=24, o3=24, ov=96, oo=24).items():
     _sb(_n, _w, "uint16")
-for _n, _w in dict(ut=512, vt=512, wt=1536, ones=512, et=2048, hb=4 * C, junk=1024, sj=8 * 192, dw=4 * C, vv=4 * C,
+for _n, _w in dict(ut=512, vt=512, w0=128, wt=1536, ones=512, et=2048, hb=4 * C, junk=1024, sj=8 * 192, dw=4 * C, vv=4 * C,
                    v64=4 * C, tf=4 * C, c2=768, c3=1024, c4=1280, c5=1536).items():
     _sb(_n, _w, "bfloat16")
 for _n, _w in dict(u=128, us=128, v=128, lay=512, k=384, e=512, h=C, m=C, f=C, d2=128, d3=192, d4=256, d5=320).items():
@@ -48,7 +48,7 @@ for _b in range(8):
     SCRATCH["p%d" % _b] = ("psum", [128, 512], "float32")
 
 BANKS = ["p%d" % b for b in range(8)]
-DMAS = ["dx", "du", "dv", "dwc", "dws", "dot", "doa", "dob"]
+DMAS = ["dx", "dx2", "du", "dv", "dwc", "dws", "dot", "doa", "dob"]
 SEMAPHORES = ["V", "S", "P", "G", "snt"] + DMAS + ["aq%d" % r for r in range(R)] + ["ao%d" % r for r in range(R)]
 
 
@@ -150,12 +150,12 @@ def rank_program(g, core, T, topo):
            ["Q" + a, "Z" + a, "Q" + b, "Z" + b, b + "0", b + "1"], [bank])
 
     def quant_halves(name, tile, state):
-        for h in range(2):
+        for h in (1, 0):
             op("V", lambda e, h=h: e.quantize_mx(T["Q" + name][:, H * h:H * h + H], T["Z" + name][:, H * h:H * h + H],
                                                  tile[:, 4 * H * h:4 * H * h + 4 * H]), state[:3] + [state[3 + h]], [name + str(h)])
 
     def mm_half(bank, a, b, h):
-        op("P", lambda e: e.matmul_mx(T[bank][:, 0:H], T["Q" + a][:], T["Z" + a][:], T["Q" + b][:, H * h:H * h + H],
+        op("P", lambda e: e.matmul_mx(T[bank][:, 0:H], T["Q" + a][:, 0:128], T["Z" + a][:, 0:128], T["Q" + b][:, H * h:H * h + H],
                                       T["Z" + b][:, H * h:H * h + H], True, True), ["Q" + a, "Z" + a, b + str(h)], [bank])
 
     def iota(name, pattern, base, cm, out=None):
@@ -172,8 +172,8 @@ def rank_program(g, core, T, topo):
     def state(r):
         return ["T%d_%s" % (r, b) for b in ("0", "1", "2", "30", "31")]
 
-    CB, CBH, CBC, CB4, TC, WV, WVB, WVP, J15 = range(9)
-    small = ["cw", "bw", "bw2", "aw", "cw2", "tau", "t1", "kw", "lt", "lf", "fa", "fb", "fc", "idx"]
+    CB, CBH, CBC, CB4, TC, WV, WVB, WVP, J15, CBD = range(10)
+    small = ["cw", "ce", "ck", "bw", "bw2", "bc", "aw", "cw2", "tau", "kw", "la", "lb", "lc", "fa", "fb", "fc", "idx"]
 
     def sm(name, a=0, b=24):
         k = 24 * small.index(name)
@@ -184,71 +184,69 @@ def rank_program(g, core, T, topo):
 
     wrap = slice(15, C, 16)
 
-    dma("Y", "dx", T.wn0[:, 0:4 * C], T.x[:], [], state(0))
+    dma("Y", "dx", T.wn0[:, 2 * C:4 * C], T.x[:, 2 * C:4 * C], [], ["T0_0", "T0_1", "T0_2", "T0_31"])
     dma("S", "du", T.ut[:], T.u[:], [], ["ut"])
-    dma("Y", "dwc", T.Qlay[:].bitcast(dt.uint8), T.wc[:], ["T0_0"], ["Qlay"])
+    dma("Y", "dx2", T.wn0[:, 0:2 * C], T.x[:, 0:2 * C], [], ["T0_30"])
+    dma("Y", "dwc", T.Qlay[:].bitcast(dt.uint8), T.wc[:], ["T0_30"], ["Qlay"])
     dma("Y", "dws", T.Zlay[:], T.ws[:], [], ["Zlay"])
     dma("Y", "dv", T.vt[:], T.v[:], [], ["vt"])
 
-    iota("vi", [[1, C]], 128, -1)
+    iota("vi", [[1, H]], 128, -1)
+    iota("wi", [[16, 8], [0, 16]], 15, -1)
     iota("pki", [[16, 8]], 8, 0, T.pki[:, 0:8])
-    iota("wi", [[16, 8], [0, 64]], 15, -1)
     iota("cw", [[16, 24]], 15, 0, sm("cw"))
-    iota("v4", [[4, L]], 131, -1)
     iota("iok", [[1, C]], 127 * 1536, 0)
+    iota("v4", [[4, L]], 131, -1)
 
-    op("V", lambda e: e.memset(T.hb[:], 0.0), [], ["hb"])
-    op("V", lambda e: e.memset(sm("cw2", 20, 24), 0.0), [], ["cw2z"])
     op("V", lambda e: e.memset(T.pw[:, 0:8], 2.0), [], ["two"])
+    op("V", lambda e: e.memset(sm("cw2", 20, 24), 0.0), [], ["cw2z"])
+    op("V", lambda e: e.memset(T.hb[:, 0:2 * C], 0.0), [], ["hb0"])
     ts(T.va[:], T.vi[:], 15, None, A.bitwise_and, None, ["vi"], ["va"])
-    cp(T.pko[:], T.pki[:, 0:8], ["pki"], ["pko"])
-    ts(T.mask[:], T.va[:], 0.0, None, A.is_equal, None, ["va"], ["mask"])
     ts(T.wsh[:], T.wi[:], 4, None, A.arith_shift_right, None, ["wi"], ["wsh"])
+    ts(T.mask[:], T.va[:], 0.0, None, A.is_equal, None, ["va"], ["mask"])
+    ts(T.w0[:], T.wsh[:], 0.0, -1.0, A.is_equal, A.mult, ["wsh"], ["w0"])
     scan(T.pw[:, 8:15], T.pw[:, 0:7], T.mask[:, 0:7], 0.5, A.mult, A.max, ["two", "mask"], ["pw1"])
-    ts(T.wt[:, 0:512], T.wsh[:], 0.0, -1.0, A.is_equal, A.mult, ["wsh"], ["w1"])
+    cp(T.pko[:], T.pki[:, 0:8], ["pki"], ["pko"])
+    ts(col(J15), T.va[:, 15:16], 1.0, None, A.mult, None, ["va"], ["j15"])
     tt(T.pw[:, 16:23], T.pw[:, 8:15], T.mask[:, 0:7], A.mult, ["pw1", "mask"], ["pw2"])
-    quant("u", T.ut[:], 128, ["ut"])
+    ts(col(CB), T.va[:, 15:16], B, None, A.mult, None, ["va"], ["cb"])
+    ts(col(CBC), T.va[:, 15:16], BC, None, A.mult, None, ["va"], ["cbc"])
     op("V", lambda e: e.tensor_reduce(col(WV), T.pw[:, 16:23], AxisListType.X, A.add), ["pw2"], ["wv"])
+    op("V", lambda e: e.memset(T.hb[:, 2 * C:4 * C], 0.0), ["hb0"], ["hb"])
+    ts(col(CBD), T.va[:, 15:16], BC, 0.125 * EMPTY, A.mult, A.add, ["va"], ["cbd"])
+    ts(sm("cw"), sm("cw"), col(J15), None, A.subtract, None, ["cw", "j15"], ["cw"])
+    quant("u", T.ut[:], 128, ["ut"])
+    ts(sm("ce"), sm("cw"), EMPTY, col(CBD), A.mult, A.add, ["cw", "cbd"], ["ce"])
+    ts(sm("ck"), sm("cw"), 1 / 256, 762.0 + 383.0, A.mult, A.add, ["cw"], ["ck"])
     cp(T.Qus[:].bitcast(dt.uint32), T.Qu[:].bitcast(dt.uint32).indirect(T.pko[:]), ["Qu", "pko"], ["Qus"])
     cp(T.Zus[:], T.Zu[:].indirect(T.pko[:]), ["Zu", "pko"], ["Zus"])
-    act(T.nmask[:], T.mask[:], F.Identity, ["mask"], ["nmask"], bias=1.0, scale=-1.0)
-    act(T.mp[:], T.mask[:], F.Identity, ["mask"], ["mp"], bias=B, scale=-18 * B)
-    act(col(WVB), col(WV), F.Identity, ["wv"], ["wvb"], scale=-73728.0)
+    for t in range(4):
+        acopy(T.wt[:, t:512:4], T.w0[:], ["w0"], ["w1%d" % t])
+    w1 = ["w1%d" % t for t in range(4)]
+    act(col(WVB), col(WV), F.Identity, ["wv"], ["wvb"], scale=-384.0)
     act(col(WVP), col(WV), F.Identity, ["wv"], ["wvp"], scale=-1536.0)
-    act(T.wt[:, 512:1024], T.wt[:, 0:512], F.Identity, ["w1", "wvb"], ["wb"], scale=col(WVB))
-    act(T.wt[:, 1024:1536], T.wt[:, 0:512], F.Identity, ["w1", "wvp"], ["wp"], scale=col(WVP))
-
-    def columns():
-        ts(col(J15), T.va[:, 15:16], 1.0, None, A.mult, None, ["va"], ["j15"])
-        ts(col(CB), T.va[:, 15:16], B, None, A.mult, None, ["va"], ["cb"])
-        ts(col(CBH), T.va[:, 15:16], B, -4064.0, A.mult, A.add, ["va"], ["cbh"])
-        ts(col(CBC), T.va[:, 15:16], BC, None, A.mult, None, ["va"], ["cbc"])
-        ts(sm("cw"), sm("cw"), col(J15), None, A.subtract, None, ["cw", "j15"], ["cw"])
-
-    def late_columns():
-        ts(T.v4a[:], T.v4[:], 2, 3, A.arith_shift_right, A.bitwise_and, ["v4"], ["v4a"])
-        ts(T.pki[:, 8:9], T.v4[:, 0:1], 3, None, A.bitwise_and, None, ["v4"], ["ti"])
-
-    def last_columns():
-        ts(T.m4a[:], T.v4a[:], 0.0, -6 * B, A.is_equal, A.mult, ["v4a"], ["m4a"])
-        ts(col(CB4), T.v4a[:, 3:4], B, None, A.mult, None, ["v4a"], ["cb4"])
-        ts(col(TC), T.pki[:, 8:9], -1.0, 3.0, A.mult, A.add, ["ti"], ["tc"])
+    act(T.nmask[:], T.mask[:], F.Identity, ["mask"], ["nmask"], bias=1.0, scale=-1.0)
+    act(T.wt[:, 512:1024], T.wt[:, 0:512], F.Identity, w1 + ["wvb"], ["wb"], scale=col(WVB))
+    act(T.wt[:, 1024:1536], T.wt[:, 0:512], F.Identity, w1 + ["wvp"], ["wp"], scale=col(WVP))
+    for h in range(2):
+        act(T.mp[:, H * h:H * h + H], T.mask[:], F.Identity, ["mask"], ["mp%d" % h], bias=B, scale=-18 * B)
+    act(T.iob[:], T.iok[:], F.Identity, ["iok"], ["iob"], scale=1 / 256)
+    mp, mc = ["mp0", "mp1"], ["mc0", "mc1"]
 
     def late_tables():
-        iota("tab2", [[192, 2 * C]], 0, 0)
+        iota("iop", [[1, 2 * C]], 0, 0)
         iota("ones", [[0, 512]], 1, 0)
         for b in range(4):
             op("G", lambda e, b=b: e.affine_select(T.et[:, 512 * b:512 * b + 512], T.ones[:], [[-1, 512]], A.is_equal, 0.0, b, 4),
                ["ones"], ["et%d" % b])
         iota("c1k", [[0, C]], 1024, 0)
         for r in range(R):
-            op("G", lambda e, r=r: e.affine_select(T["xt%d" % r][:, C:3 * C], T.tab2[:], [[0, 2 * C]], A.is_gt, EMPTY, -1, 0),
-               ["tab2"], ["tq%d" % r])
+            op("G", lambda e, r=r: e.affine_select(T["xt%d" % r][:, C:3 * C], T.iop[:], [[0, 2 * C]], A.is_gt, EMPTY, -1, 0),
+               ["iop"], ["tq%d" % r])
             if r == 0:
                 iota("k3c", [[-511, C]], 0, 0)
-        iota("iop", [[1, 480]], 0, 0)
 
-    def ranking(nv, row_v, row_s, res_v, res_s, scalar, res_k, early, later):
+    def ranking(nv, row_v, row_s, res_v, res_s, scalar, res_k, early, later, last, narrow_first=False):
         def dest(c):
             w = WIDTH[c]
             if c < 8:
@@ -269,16 +267,19 @@ def rank_program(g, core, T, topo):
 
         def row(c):
             out, name = dest(c)
-            ts(out, row_v(WIDTH[c]), scalar(c), 2.0, A.is_lt, A.mult, res_k + res_v[0], [name] + res_v[1])
+            ts(out, row_v(WIDTH[c]), scalar(c), 2.0, A.is_lt, A.mult, res_k(c) + res_v[0], [name] + res_v[1])
 
-        for c in range(23 - nv, -1, -1):
+        order = list(range(23 - nv, -1, -1))
+        if narrow_first:
+            order = [11, 10] + [c for c in order if c not in (11, 10)]
+        for c in order:
             out, name = dest(c)
-            act(out, row_s(WIDTH[c]), F.Sign, res_k + res_s[0], [name, "aw%d" % c] + res_s[1], bias=scalar(c), scale=-1.0,
+            act(out, row_s(WIDTH[c]), F.Sign, res_k(c) + res_s[0], [name, "aw%d" % c] + res_s[1], bias=scalar(c), scale=-1.0,
                 accum=sm("aw", c, c + 1))
         row(23)
         for f in early:
             f()
-        for c in range(22, max(19, 23 - nv), -1):
+        for c in range(22, 19, -1):
             row(c)
         todo = list(range(23, 23 - nv, -1))
         if nv > 4:
@@ -303,20 +304,15 @@ def rank_program(g, core, T, topo):
         for c in todo[:3]:
             sums(c)
         k = 192 * (24 - nv - 16) + 191
-
-        def own():
-            ts(sm("aw", 24 - nv, 24), T.sj[:, k:8 * 192:192], 1.0, None, A.add, None,
-               ["sj%d" % c for c in range(24 - nv, 24)], ["aw%d" % c for c in range(24 - nv, 24)])
-
-        latch(T.colw[:], T.mp[:, 0:320], T.p5[:, 0:320], ["mp"], ["colw", "p5"])
+        latch(T.colw[:], T.mp[:, 0:320], T.p5[:, 0:320], mp, ["colw", "p5"])
         for c in todo[3:]:
             sums(c)
-        if not todo[3:]:
-            own()
         ts(sm("cw2", 0, 16), T.colw[:, 15:256:16], col(CB), 16.0 * nv, A.subtract, A.add, ["colw", "cb"], ["cw2a"])
-        ts(sm("cw2", 16, 20), T.colw[:, 271:320:16], col(CB), 16.0 * min(nv, 4), A.subtract, A.add, ["colw", "cb"], ["cw2b"])
-        if todo[3:]:
-            own()
+        ts(sm("cw2", 16, 20), T.colw[:, 271:320:16], col(CB), 64.0, A.subtract, A.add, ["colw", "cb"], ["cw2b"])
+        ts(sm("aw", 24 - nv, 24), T.sj[:, k:8 * 192:192], 1.0, None, A.add, None,
+           ["sj%d" % c for c in range(24 - nv, 24)], ["aw%d" % c for c in range(24 - nv, 24)])
+        for f in last:
+            f()
         tt(sm("tau"), sm("aw"), sm("cw2"), A.add, ["aw%d" % c for c in range(24)] + ["cw2a", "cw2b", "cw2z"], ["tau"])
 
     for r in range(R):
@@ -330,95 +326,117 @@ def rank_program(g, core, T, topo):
         arrive(src, "aq%d" % r, 2, ["Q" + ql, "Z" + ql])
         if r == 0:
             late_tables()
-        mm_half("p6", "us", qt, 0)
         mm_half("p7", "us", qt, 1)
+        mm_half("p6", "us", qt, 0)
         mm("p2", "u", 0, qt, C)
         mm("p0", "us", 0, qt, C)
         mm("p1", "us", 0, qt, C)
         if r == 0:
-            columns()
-        tt(T.mk[:, 0:H], T.p6[:, 0:H], T.mask[:, 0:H], A.mult, ["mask"], ["mka", "p6"])
-        tt(T.mk[:, H:C], T.p7[:, 0:H], T.mask[:, 0:H], A.mult, ["mask"], ["mkb", "p7"])
-        act(T.hb[:, 0:4 * C:4], T.p2[:, 0:C], F.Sign, [], ["hb", "p2"], bias=-TINY)
-        scan(T.sw[:], T.nmask[:], T.mk[:], 0.0, A.mult, A.add, ["nmask", "mka", "mkb"], ["sw"])
+            quant("k", T.wt[:], 384, w1 + ["wb", "wp"])
+        tt(T.mk[:, H:C], T.p7[:, 0:H], T.mask[:], A.mult, ["mask"], ["mk1", "p7"])
+        tt(T.mk[:, 0:H], T.p6[:, 0:H], T.mask[:], A.mult, ["mask"], ["mk0", "p6"])
+        for h in (1, 0):
+            scan(T.sw[:, H * h:H * h + H], T.nmask[:], T.mk[:, H * h:H * h + H], 0.0, A.mult, A.add, ["nmask", "mk%d" % h], ["sw%d" % h])
 
         def homes():
-            if r == 0:
-                quant("k", T.wt[:], 384, ["w1", "wb", "wp"])
             quant("h", T.hb[:], C, ["hb"])
             mm("p4", "k", 256, "h", C)
             mm("p3", "k", 128, "h", C)
 
         def home_keys():
-            latch(T.hw[:], T.mp[:], T.p4[:, 0:C], ["mp"], ["hw", "p4"])
-            tt(T.brow[:], T.p3[:, 0:C], T.iok[:], A.add, ["iok"], ["brow", "p3"])
-            ts(sm("bw"), T.hw[:, wrap], col(CBH), 48.0, A.subtract, A.mult, ["hw", "cbh"], ["bw"])
+            latch(T.hw[:], T.mp[:], T.p4[:, 0:C], mp, ["hw", "p4"])
+            tt(T.brow[:], T.p3[:, 0:C], T.iob[:], A.add, ["iob"], ["brow", "p3"])
+            ts(sm("bw"), T.hw[:, wrap], col(CB), 0.25, A.subtract, A.mult, ["hw", "cb"], ["bw"])
 
         def home_wrap():
-            tt(sm("bw2"), sm("bw"), sm("cw"), A.add, ["bw", "cw"], ["bw2"])
+            tt(sm("bw2"), sm("bw"), sm("ck"), A.add, ["bw", "ck"], ["bw2"])
 
         def packed():
             tt(T.prow[:], T.p4[:, 0:C], T.iok[:], A.add, ["iok"], ["prow", "p4"])
 
+        def key_base():
+            tt(sm("bc"), sm("bw2"), sm("cw2"), A.subtract, ["bw2", "cw2a", "cw2b", "cw2z"], ["bc"])
+
+        act(T.hb[:, 0:4 * C:4], T.p2[:, 0:C], F.Sign, [], ["hb", "p2"], bias=-TINY)
         ranking(NV[0], lambda w: T.p0[:, 0:w], lambda w: T.p1[:, 0:w], ([], ["p0"]), ([], ["p1"]),
-                lambda c: T.sw[:, 16 * c + 15:16 * c + 16], ["sw"], [homes], [home_keys, packed, home_wrap])
+                lambda c: T.sw[:, 16 * c + 15:16 * c + 16], lambda c: ["sw%d" % (c // 12)], [homes],
+                [home_keys, packed, home_wrap], [key_base])
+        tt(sm("kw"), sm("bc"), sm("aw"), A.subtract, ["bc"] + ["aw%d" % c for c in range(24)], ["kw"])
         ts(T.o1[:], sm("tau"), -1.0, 383.0, A.mult, A.add, ["tau"], ["o1"])
-        act(sm("t1"), sm("tau"), F.Identity, ["tau"], ["t1"], bias=192.0 * 383, scale=-192.0)
-        tt(T.krow[:], T.tab2[:].indirect(T.o1[:]), T.brow[:], A.add, ["tab2", "o1", "brow"], ["krow"])
-        tt(sm("kw"), sm("t1"), sm("bw2"), A.add, ["t1", "bw2"], ["kw"])
+        if r == 0:
+            ts(T.v4a[:], T.v4[:], 2, 3, A.arith_shift_right, A.bitwise_and, ["v4"], ["v4a"])
+        for h in range(2):
+            tt(T.krow[:, H * h:H * h + H], T.iop[:].indirect(T.o1[:, 12 * h:12 * h + 12]), T.brow[:, H * h:H * h + H], A.add,
+               ["iop", "o1", "brow"], ["krow%d" % h])
+        if r == 0:
+            ts(T.m4[:, L:2 * L], T.v4a[:], 0.0, -6 * B, A.is_equal, A.mult, ["v4a"], ["m4a"])
         banks = ["p2", "p6", "p7", "p0"]
 
         def unpack():
             for b in range(4):
                 mm(banks[b], "e", 128 * b, ql, C)
 
-        def ident():
-            quant("e", T.et[:], 512, ["et%d" % b for b in range(4)])
+        def ident(b):
+            op("V", lambda e: e.quantize_mx(T.Qe[:, 128 * b:128 * b + 128], T.Ze[:, 128 * b:128 * b + 128],
+                                            T.et[:, 512 * b:512 * b + 512]), ["et%d" % b], ["Qe%d" % b] + (["Qe", "Ze"] if b == 3 else []))
 
         if r > 0:
             unpack()
-        ranking(NV[1], lambda w: T.krow[:, 0:w], lambda w: T.krow[:, 0:w], (["krow"], []), (["krow"], []),
-                lambda c: sm("kw", c, c + 1), ["kw"], [], [late_columns, last_columns, ident] if r == 0 else [])
+        ranking(NV[1], lambda w: T.krow[:, 0:w], lambda w: T.krow[:, 0:w], ([], []), ([], []), lambda c: sm("kw", c, c + 1),
+                lambda c: ["kw", "krow0"] + (["krow1"] if WIDTH[c] > H else []), [], [], [], True)
+        if r == 0:
+            ident(0)
         ts(T.o2[:], sm("tau"), 383.0, 0.5, A.add, A.mult, ["tau"], ["o2"])
+        if r == 0:
+            ident(1)
         cp(T.ps[:].indirect(T.o2[:]), T.prow[:], ["prow", "o2"], ["ps"])
         if r == 0:
+            ident(2)
+            for h in range(2):
+                act(T.mc[:, H * h:H * h + H], T.mask[:], F.Identity, ["mask"], ["mc%d" % h], bias=BC, scale=-18 * BC)
+            act(T.m4[:, 0:L], T.m4[:, L:2 * L], F.Identity, ["m4a"], ["m4"], bias=B)
+        scan(T.qs[:], T.c1k[:], T.ps[:], -4096.0, A.add, A.max, ["c1k", "ps"], ["qs"])
+        if r == 0:
+            ident(3)
             unpack()
-            act(T.mc[:], T.mask[:], F.Identity, ["mask"], ["mc"], bias=BC, scale=-18 * BC)
-            act(T.m4[:], T.m4a[:], F.Identity, ["m4a"], ["m4"], bias=B)
         for b in range(4):
             acopy(T.dw[:, b:4 * C:4], T[banks[b]][:, 0:C], [], ["dw%d" % b, banks[b]])
-        scan(T.qs[:], T.c1k[:], T.ps[:], -4096.0, A.add, A.max, ["c1k", "ps"], ["qs"])
-        latch(T.qw[:], T.mp[:], T.qs[:], ["mp", "qs"], ["qw"])
+        latch(T.qw[:], T.mp[:], T.qs[:], mp + ["qs"], ["qw"])
+        if r == 0:
+            ts(T.pki[:, 8:9], T.v4[:, 0:1], 3, None, A.bitwise_and, None, ["v4"], ["ti"])
+            ts(col(CB4), T.v4a[:, 3:4], B, None, A.mult, None, ["v4a"], ["cb4"])
         ts(T.oq[:], T.qw[:, wrap], col(CB), 1 / 1024, A.subtract, A.mult, ["qw", "cb"], ["oq"])
+        if r == 0:
+            ts(col(TC), T.pki[:, 8:9], -1.0, 3.0, A.mult, A.add, ["ti"], ["tc"])
         cp(xt[:, C:3 * C].indirect(T.oq[:]), T.ps[:], ["ps", "oq"], [tq])
         act(T.tr1[:], xt[:, C:3 * C], F.Identity, [tq], ["tr1"], bias=MAGIC)
         act(T.tr2[:, 0:C], T.tr1[:, 0:C], F.Identity, ["tr1"], ["tr2a"], bias=-MAGIC / 2, scale=0.5)
         act(T.tr2[:, C:2 * C], T.tr1[:, C:2 * C], F.Identity, ["tr1"], ["tr2b"], bias=-MAGIC / 2 - 384 * 512, scale=0.5)
-        scan(xt[:, 0:C], xt[:, C:2 * C], T.c1k[:], 383 * EMPTY, A.add, A.max, [tq, "c1k"], ["cum%d" % r])
-        latch(T.xw[:, C:2 * C], T.mc[:], xt[:, C:2 * C], ["mc", tq], ["xwb"])
-        latch(T.xw[:, 0:C], T.mc[:], xt[:, 0:C], ["mc", "cum%d" % r], ["xwa"])
-        ts(T.y48[:], T.xw[:, 15:2 * C:16], col(CBC), 1 / EMPTY, A.subtract, A.mult, ["xwa", "xwb", "cbc"], ["y48"])
-        tt(sm("lt"), T.y48[:, 0:24], T.y48[:, 24:48], A.mult, ["y48"], ["lt"])
-        tt(sm("lf"), sm("lt"), sm("cw"), A.max, ["lt", "cw"], ["lf"])
-        ts(T.ol[:], sm("lf"), 0.25, None, A.add, None, ["lf"], ["ol"])
+        latch(T.xw[:, C:2 * C], T.mc[:], xt[:, C:2 * C], mc + [tq], ["xwb"])
+        scan(xt[:, 0:C], xt[:, C:2 * C], T.c1k[:], 383.125 * EMPTY, A.add, A.max, [tq, "c1k"], ["cum%d" % r])
+        ts(sm("la"), T.xw[:, C + 15:2 * C:16], col(CBC), 1024.0, A.subtract, A.mult, ["xwb", "cbc"], ["la"])
+        latch(T.xw[:, 0:C], T.mc[:], xt[:, 0:C], mc + ["cum%d" % r], ["xwa"])
+        tt(sm("lb"), sm("la"), sm("ce"), A.add, ["la", "ce"], ["lb"])
+        tt(sm("lc"), sm("lb"), T.xw[:, wrap], A.min, ["lb", "xwa"], ["lc"])
+        ts(T.ol[:], sm("lc"), col(CBC), 1 / EMPTY, A.subtract, A.mult, ["lc", "cbc"], ["ol"])
         tt(T.k3[:], T.tr2[:].indirect(T.ol[:]), T.k3c[:], A.add, ["tr2a", "tr2b", "ol", "k3c"], ["k3"])
         acopy(T.grow[:], xt[:, C:3 * C].indirect(T.ol[:]), [tq, "ol"], ["grow"])
-        latch(T.k3s[:], T.mp[:], T.k3[:], ["mp", "k3"], ["k3s"])
+        latch(T.k3s[:], T.mp[:], T.k3[:], mp + ["k3"], ["k3s"])
         act(T.k3r[:], T.k3[:], F.Identity, ["k3", "cb"], ["k3r"], bias=col(CB))
         ranking(NV[2], lambda w: T.k3r[:, 0:w], lambda w: T.k3r[:, 0:w], (["k3r"], []), (["k3r"], []),
-                lambda c: T.k3s[:, 16 * c + 15:16 * c + 16], ["k3s"], [], [])
+                lambda c: T.k3s[:, 16 * c + 15:16 * c + 16], lambda c: ["k3s"], [], [], [])
         ts(T.o3[:], sm("tau"), 383.0, 0.5, A.add, A.mult, ["tau"], ["o3"])
         ts(sm("fa"), sm("tau"), -191.0, None, A.is_lt, None, ["tau"], ["fa"])
         cp(T.bl[:].indirect(T.o3[:]), T.grow[:], ["grow", "o3"], ["bl"])
         ts(sm("fb"), sm("tau"), 1151.0, 0.5, A.add, A.mult, ["tau"], ["fb"])
-        latch(T.b4[:], T.m4[:], T.bl[:, 0:L], ["m4", "bl"], ["b4"])
+        latch(T.b4[:], T.m4[:, 0:L], T.bl[:, 0:L], ["m4", "bl"], ["b4"])
         ts(si(0), T.b4[:, 3:L:4], col(CB4), None, A.subtract, None, ["b4", "cb4"], ["bi"])
         ts(si(1), si(0), 1023, None, A.bitwise_and, None, ["bi"], ["bj"])
         ob, oa = T["ob%d" % r], T["oa%d" % r]
         ts(ob[:], si(1), 4.0, col(TC), A.mult, A.add, ["bj", "tc"], ["ob%d" % r])
         send(dst, "ao%d" % r, oa[:], ob[:], ["ob%d" % r])
         arrive(src, "ao%d" % r, 1, ["oa%d" % r])
-        latch(T.gw[:], T.mp[:], T.grow[:], ["mp", "grow"], ["gw"])
+        latch(T.gw[:], T.mp[:], T.grow[:], mp + ["grow"], ["gw"])
         tt(sm("fc"), sm("fa"), sm("fb"), A.mult, ["fa", "fb"], ["fc"])
         ts(si(2), T.gw[:, wrap], col(CB), None, A.subtract, None, ["gw", "cb"], ["mi"])
         ts(si(3), si(2), 1023, None, A.bitwise_and, None, ["mi"], ["mj"])
@@ -437,29 +455,36 @@ def rank_program(g, core, T, topo):
         win = tn + ["Ba%d" % r, "Bb%d" % r]
         for t in range(4):
             (cp if t < 2 else acopy)(T.vv[:, t:4 * C:4], wn[:].indirect(T.ov[:, 24 * t:24 * t + 24]), win + ["ov%d" % t], ["vv%d" % t])
-        quant("m", T.vv[:], C, ["vv%d" % t for t in range(4)])
-        rb = ["p0", "p1", "p3", "p4"]
-        for b in (0, 3, 1, 2):
-            mm(rb[b], "lay", 128 * b, "m", C)
+        quant_halves("m", T.vv, ["vv0", "vv1", "vv2", "vv3", "vv3"])
         ts(T.v64[:, 0:C], T.vv[:, 0:4 * C:4], 64.0, None, A.mult, None, ["vv0"], ["v640"])
+        mm_half("p5", "lay", "m", 1)
+        mm_half("p2", "lay", "m", 0)
+        rb = ["p0", "p1", "p3", "p4"]
+        for b in (3, 1, 2):
+            mm(rb[b], "lay", 128 * b, "m", C)
         for b in (2, 1):
             act(T.v64[:, C * b:C * b + C], T.vv[:, b:4 * C:4], F.Identity, ["vv%d" % b], ["v64%d" % b], scale=64.0)
         act(T.tmp[:, 3 * C:4 * C], T.p4[:, 0:C], F.Identity, [], ["tmp3", "p4"], scale=0.015625)
         new = T["wn%d" % (r + 1)] if r + 1 < R else T.tf
         for b in range(3):
-            tt(T.tmp[:, C * b:C * b + C], T[rb[b]][:, 0:C], T.v64[:, C * b:C * b + C], A.add, ["v64%d" % b], ["tmp%d" % b, rb[b]])
-            act(new[:, b:4 * C:4], T.tmp[:, C * b:C * b + C], F.Identity, ["tmp%d" % b], ["T%d_%d" % (r + 1, b)], scale=0.015625)
-        for h in range(2):
+            if b == 0:
+                tt(T.tmp[:, H:C], T.p5[:, 0:H], T.v64[:, H:C], A.add, ["v640"], ["tmp0h", "p5"])
+                tt(T.tmp[:, 0:H], T.p2[:, 0:H], T.v64[:, 0:H], A.add, ["v640"], ["tmp0", "p2"])
+            else:
+                tt(T.tmp[:, C * b:C * b + C], T[rb[b]][:, 0:C], T.v64[:, C * b:C * b + C], A.add, ["v64%d" % b], ["tmp%d" % b, rb[b]])
+            act(new[:, b:4 * C:4], T.tmp[:, C * b:C * b + C], F.Identity, ["tmp%d" % b, "tmp0h"], ["T%d_%d" % (r + 1, b)], scale=0.015625)
+        for h in (1, 0):
             tt(new[:, 4 * H * h + 3:4 * H * h + 4 * H:4], T.tmp[:, 3 * C + H * h:3 * C + H * h + H],
                T.vv[:, 4 * H * h + 3:4 * H * h + 4 * H:4], A.add, ["tmp3", "vv3"], ["T%d_3%d" % (r + 1, h)])
 
     quant_halves("f", T.tf, state(R))
-    mm_half("p6", "v", "f", 0)
     mm_half("p7", "v", "f", 1)
+    mm_half("p6", "v", "f", 0)
     dma("Y", "doa", T.oc[:], T.Qf[:].bitcast(dt.uint8), ["f0", "f1"], [])
-    cp(T.yo[:, 0:H], T.p6[:, 0:H], [], ["ya", "p6"])
     cp(T.yo[:, H:C], T.p7[:, 0:H], [], ["yb", "p7"])
+    cp(T.yo[:, 0:H], T.p6[:, 0:H], [], ["ya", "p6"])
     for k in range(4):
         dma("S" if k < 2 else "Y", "dob" if k < 2 else "doa", T.osc[4 * k:4 * k + 4, :], T.Zf[32 * k:32 * k + 4, :], ["f0", "f1"], [])
-    dma("S", "dob", T.y[:], T.yo[:], ["ya", "yb"], [])
+    dma("S", "dob", T.y[:, H:C], T.yo[:, H:C], ["yb"], [])
+    dma("Y", "doa", T.y[:, 0:H], T.yo[:, 0:H], ["ya"], [])
     _emit(g, T, ops)

from concourse.mybir import dt, AluOpType, AxisListType, ActivationFunctionType

A = AluOpType
F = ActivationFunctionType
C, L, R = 384, 96, 3
H = C // 2
STEP = [1, 2, 4]
X4 = "float8_e4m3fn_x4"
B = float(2 ** 20)
BC = float(2 ** 42)
EMPTY = float(2 ** 32)
MAGIC = 1.5 * 2 ** 33
TINY = 2.0 ** -120
NV = [4, 6, 6]
WIDTH = [128] * 8 + [192] * 4 + [256] * 4 + [320] * 4 + [384] * 4

SCRATCH = {}


def _sb(name, n, dtype):
    SCRATCH[name] = ("sbuf", [128, n], dtype)


for _n, _w in dict(mask=H, nmask=H, mp=C, mc=C, m4=2 * L, cols=16, pw=32, iok=C, iob=C, iop=2 * C, k3c=C,
                   c1k=C, mk=C, sw=C, brow=C, prow=C, hw=C, sm=24 * 18, colw=320, krow=C,
                   ps=C, qs=C, qw=C, xw=2 * C, tr1=2 * C, tr2=2 * C, grow=C, k3=C, k3s=C, k3r=C,
                   bl=C, b4=L, gw=C, tmp=4 * C, yo=C, otr=C).items():
    _sb(_n, _w, "float32")
for _n, _w in dict(vi=H, va=H, pki=16, wi=128, wsh=128, v4=L, v4a=L, si=24 * 4).items():
    _sb(_n, _w, "int32")
for _n, _w in dict(pko=8, o1=24, o2=24, oq=24, ol=24, o3=24, ov=96, oo=24).items():
    _sb(_n, _w, "uint16")
for _n, _w in dict(ut=512, vt=512, w0=128, wt=1536, ones=512, et=2048, hb=4 * C, junk=1024, sj=8 * 192, dw=4 * C, vv=4 * C,
                   v64=4 * C, tf=4 * C, c2=768, c3=1024, c4=1280, c5=1536).items():
    _sb(_n, _w, "bfloat16")
for _n, _w in dict(u=128, us=128, v=128, lay=512, k=384, e=512, h=C, m=C, f=C, d2=128, d3=192, d4=256, d5=320).items():
    _sb("Q" + _n, _w, X4)
    _sb("Z" + _n, _w, "uint8")
for _r in range(R):
    _sb("wn%d" % _r, 4 * (C + L), "bfloat16")
    _sb("xt%d" % _r, 3 * C, "float32")
    for _n in ("t", "l"):
        _sb("Q%s%d" % (_n, _r), C, X4)
        _sb("Z%s%d" % (_n, _r), C, "uint8")
    _sb("ob%d" % _r, 24, "uint16")
    _sb("oa%d" % _r, 24, "uint16")
for _b in range(8):
    SCRATCH["p%d" % _b] = ("psum", [128, 512], "float32")

BANKS = ["p%d" % b for b in range(8)]
DMAS = ["dx", "dx2", "du", "dv", "dwc", "dws", "dot", "doa", "dob"]
SEMAPHORES = ["V", "S", "P", "G", "snt"] + DMAS + ["aq%d" % r for r in range(R)] + ["ao%d" % r for r in range(R)]


def _emit(g, T, ops):
    queue = {"V": g.vector, "S": g.scalar, "P": g.tensor, "G": g, "Y": g.sync}
    count, writer, readers = {}, {}, {}
    known = {q: {} for q in queue}
    for q, sem, inc, fn, reads, writes in ops:
        deps = []
        for x in reads:
            if x in writer:
                deps.append(writer[x])
        for x in writes:
            if x in writer and not (x in BANKS and writer[x][0] == q):
                deps.append(writer[x])
            deps.extend(readers.get(x, []))
        if fn is not None:
            need = {}
            for s, k, clock in deps:
                if known[q].get(s, 0) < k and need.get(s, (0, None))[0] < k:
                    need[s] = (k, clock)
            for s in sorted(need, key=lambda s: -sum(need[s][1].values())):
                k, clock = need[s]
                if known[q].get(s, 0) >= k:
                    continue
                queue[q].wait_ge(T.sem[s], k)
                known[q][s] = k
                for s2, k2 in clock.items():
                    if known[q].get(s2, 0) < k2:
                        known[q][s2] = k2
            ins = fn(queue[q])
            if sem != "snt":
                ins.then_inc(T.sem[sem], inc)
        count[sem] = count.get(sem, 0) + inc
        if sem == "snt":
            continue
        me = (sem, count[sem], dict(known[q]) if fn is not None else {})
        for x in reads:
            readers.setdefault(x, []).append(me)
        for x in writes:
            writer[x] = me
            readers[x] = []
    for s in sorted(count):
        g.wait_ge(T.sem[s], count[s])


def rank_program(g, core, T, topo):
    rank = T.rank_of(core)
    if rank is None:
        return
    n = len(T.cores)
    ops = []

    def op(q, fn, reads, writes):
        ops.append((q, q, 1, fn, reads, writes))

    def dma(q, sem, out, in_, reads, writes):
        ops.append((q, sem, 16, lambda e: e.dma_start(out, in_), reads, writes))

    def send(dst, sem, out, in_, reads):
        rid, pid, _ = topo.addr(dst)
        m = topo.mask(core, dst)
        ops.append(("G", "snt", len(topo.engines(core, dst)),
                    lambda e: e.remote_dma(out, in_, T.sem[sem], T.sem.snt, pid, rid, m), reads, []))

    def arrive(src, sem, k, writes):
        ops.append(("G", sem, k * len(topo.engines(src, core)), None, [], writes))

    def ts(out, in0, s1, s2, op0, op1, reads, writes):
        if op1 is None:
            op("V", lambda e: e.tensor_scalar(out, in0, s1, None, op0), reads, writes)
        else:
            op("V", lambda e: e.tensor_scalar(out, in0, s1, s2, op0, op1), reads, writes)

    def tt(out, in0, in1, o, reads, writes):
        op("V", lambda e: e.tensor_tensor(out, in0, in1, o), reads, writes)

    def cp(out, in_, reads, writes):
        op("V", lambda e: e.tensor_copy(out, in_), reads, writes)

    def scan(out, d0, d1, init, op0, op1, reads, writes):
        op("V", lambda e: e.tensor_tensor_scan(out, d0, d1, init, op0, op1), reads, writes)

    def latch(out, m, src, reads, writes):
        scan(out, m, src, 0.0, A.add, A.max, reads, writes)

    def act(out, in_, func, reads, writes, bias=0.0, scale=1.0, accum=None):
        op("S", lambda e: e.activation(out, in_, func, bias=bias, scale=scale, accum_out=accum), reads, writes)

    def acopy(out, in_, reads, writes):
        op("S", lambda e: e.activation(out, in_, F.Copy), reads, writes)

    def quant(name, in_, w, reads):
        op("V", lambda e: e.quantize_mx(T["Q" + name][:, 0:w], T["Z" + name][:, 0:w], in_), reads, ["Q" + name, "Z" + name])

    def mm(bank, a, a0, b, w, start=True, stop=True):
        op("P", lambda e: e.matmul_mx(T[bank][:, 0:w], T["Q" + a][:, a0:a0 + 128], T["Z" + a][:, a0:a0 + 128],
                                      T["Q" + b][:, 0:w], T["Z" + b][:, 0:w], start, stop),
           ["Q" + a, "Z" + a, "Q" + b, "Z" + b, b + "0", b + "1"], [bank])

    def quant_halves(name, tile, state):
        for h in (1, 0):
            op("V", lambda e, h=h: e.quantize_mx(T["Q" + name][:, H * h:H * h + H], T["Z" + name][:, H * h:H * h + H],
                                                 tile[:, 4 * H * h:4 * H * h + 4 * H]), state[:3] + [state[3 + h]], [name + str(h)])

    def mm_half(bank, a, b, h):
        op("P", lambda e: e.matmul_mx(T[bank][:, 0:H], T["Q" + a][:, 0:128], T["Z" + a][:, 0:128], T["Q" + b][:, H * h:H * h + H],
                                      T["Z" + b][:, H * h:H * h + H], True, True), ["Q" + a, "Z" + a, b + str(h)], [bank])

    def iota(name, pattern, base, cm, out=None):
        if out is None:
            out = T[name][:]
        if name in ("vi", "pki", "wi", "v4"):
            op("G", lambda e: e.iota(out, pattern, base, cm), [], [name])
        else:
            op("G", lambda e: e.iota(out, pattern, base, cm, allow_small_or_imprecise_dtypes=True), [], [name])

    def col(k):
        return T.cols[:, k:k + 1]

    def state(r):
        return ["T%d_%s" % (r, b) for b in ("0", "1", "2", "30", "31")]

    CB, CBH, CBC, CB4, TC, WV, WVB, WVP, J15, CBD = range(10)
    small = ["cw", "ce", "ck", "bw", "bw2", "bc", "aw", "cw2", "tau", "kw", "la", "lb", "lc", "fa", "fb", "fc", "idx"]

    def sm(name, a=0, b=24):
        k = 24 * small.index(name)
        return T.sm[:, k + a:k + b]

    def si(k):
        return T.si[:, 24 * k:24 * k + 24]

    wrap = slice(15, C, 16)

    dma("Y", "dx", T.wn0[:, 2 * C:4 * C], T.x[:, 2 * C:4 * C], [], ["T0_0", "T0_1", "T0_2", "T0_31"])
    dma("S", "du", T.ut[:], T.u[:], [], ["ut"])
    dma("Y", "dx2", T.wn0[:, 0:2 * C], T.x[:, 0:2 * C], [], ["T0_30"])
    dma("Y", "dwc", T.Qlay[:].bitcast(dt.uint8), T.wc[:], ["T0_30"], ["Qlay"])
    dma("Y", "dws", T.Zlay[:], T.ws[:], [], ["Zlay"])
    dma("Y", "dv", T.vt[:], T.v[:], [], ["vt"])

    iota("vi", [[1, H]], 128, -1)
    iota("wi", [[16, 8], [0, 16]], 15, -1)
    iota("pki", [[16, 8]], 8, 0, T.pki[:, 0:8])
    iota("cw", [[16, 24]], 15, 0, sm("cw"))
    iota("iok", [[1, C]], 127 * 1536, 0)
    iota("v4", [[4, L]], 131, -1)

    op("V", lambda e: e.memset(T.pw[:, 0:8], 2.0), [], ["two"])
    op("V", lambda e: e.memset(sm("cw2", 20, 24), 0.0), [], ["cw2z"])
    op("V", lambda e: e.memset(T.hb[:, 0:2 * C], 0.0), [], ["hb0"])
    ts(T.va[:], T.vi[:], 15, None, A.bitwise_and, None, ["vi"], ["va"])
    ts(T.wsh[:], T.wi[:], 4, None, A.arith_shift_right, None, ["wi"], ["wsh"])
    ts(T.mask[:], T.va[:], 0.0, None, A.is_equal, None, ["va"], ["mask"])
    ts(T.w0[:], T.wsh[:], 0.0, -1.0, A.is_equal, A.mult, ["wsh"], ["w0"])
    scan(T.pw[:, 8:15], T.pw[:, 0:7], T.mask[:, 0:7], 0.5, A.mult, A.max, ["two", "mask"], ["pw1"])
    cp(T.pko[:], T.pki[:, 0:8], ["pki"], ["pko"])
    ts(col(J15), T.va[:, 15:16], 1.0, None, A.mult, None, ["va"], ["j15"])
    tt(T.pw[:, 16:23], T.pw[:, 8:15], T.mask[:, 0:7], A.mult, ["pw1", "mask"], ["pw2"])
    ts(col(CB), T.va[:, 15:16], B, None, A.mult, None, ["va"], ["cb"])
    ts(col(CBC), T.va[:, 15:16], BC, None, A.mult, None, ["va"], ["cbc"])
    op("V", lambda e: e.tensor_reduce(col(WV), T.pw[:, 16:23], AxisListType.X, A.add), ["pw2"], ["wv"])
    op("V", lambda e: e.memset(T.hb[:, 2 * C:4 * C], 0.0), ["hb0"], ["hb"])
    ts(col(CBD), T.va[:, 15:16], BC, 0.125 * EMPTY, A.mult, A.add, ["va"], ["cbd"])
    ts(sm("cw"), sm("cw"), col(J15), None, A.subtract, None, ["cw", "j15"], ["cw"])
    quant("u", T.ut[:], 128, ["ut"])
    ts(sm("ce"), sm("cw"), EMPTY, col(CBD), A.mult, A.add, ["cw", "cbd"], ["ce"])
    ts(sm("ck"), sm("cw"), 1 / 256, 762.0 + 383.0, A.mult, A.add, ["cw"], ["ck"])
    cp(T.Qus[:].bitcast(dt.uint32), T.Qu[:].bitcast(dt.uint32).indirect(T.pko[:]), ["Qu", "pko"], ["Qus"])
    cp(T.Zus[:], T.Zu[:].indirect(T.pko[:]), ["Zu", "pko"], ["Zus"])
    for t in range(4):
        acopy(T.wt[:, t:512:4], T.w0[:], ["w0"], ["w1%d" % t])
    w1 = ["w1%d" % t for t in range(4)]
    act(col(WVB), col(WV), F.Identity, ["wv"], ["wvb"], scale=-384.0)
    act(col(WVP), col(WV), F.Identity, ["wv"], ["wvp"], scale=-1536.0)
    act(T.nmask[:], T.mask[:], F.Identity, ["mask"], ["nmask"], bias=1.0, scale=-1.0)
    act(T.wt[:, 512:1024], T.wt[:, 0:512], F.Identity, w1 + ["wvb"], ["wb"], scale=col(WVB))
    act(T.wt[:, 1024:1536], T.wt[:, 0:512], F.Identity, w1 + ["wvp"], ["wp"], scale=col(WVP))
    for h in range(2):
        act(T.mp[:, H * h:H * h + H], T.mask[:], F.Identity, ["mask"], ["mp%d" % h], bias=B, scale=-18 * B)
    act(T.iob[:], T.iok[:], F.Identity, ["iok"], ["iob"], scale=1 / 256)
    mp, mc = ["mp0", "mp1"], ["mc0", "mc1"]

    def late_tables():
        iota("iop", [[1, 2 * C]], 0, 0)
        iota("ones", [[0, 512]], 1, 0)
        for b in range(4):
            op("G", lambda e, b=b: e.affine_select(T.et[:, 512 * b:512 * b + 512], T.ones[:], [[-1, 512]], A.is_equal, 0.0, b, 4),
               ["ones"], ["et%d" % b])
        iota("c1k", [[0, C]], 1024, 0)
        for r in range(R):
            op("G", lambda e, r=r: e.affine_select(T["xt%d" % r][:, C:3 * C], T.iop[:], [[0, 2 * C]], A.is_gt, EMPTY, -1, 0),
               ["iop"], ["tq%d" % r])
            if r == 0:
                iota("k3c", [[-511, C]], 0, 0)

    def ranking(nv, row_v, row_s, res_v, res_s, scalar, res_k, early, later, last, narrow_first=False):
        def dest(c):
            w = WIDTH[c]
            if c < 8:
                return T.junk[:, 128 * c:128 * c + 128], "j%d" % c
            return T["c%d" % (c // 4)][:, c % 4:4 * w:4], "c%d" % c

        def cols_of(u, first):
            w = WIDTH[4 * u] - 64
            quant("d%d" % u, T["c%d" % u][:, 0:4 * w], w, ["c%d" % c for c in range(4 * u, 4 * u + 4)])
            mm("p5", "k", 0, "d%d" % u, w, first, u == 2)

        def sums(c):
            w = WIDTH[c]
            k = 192 * (c - 16) + 192
            t = T["c%d" % (c // 4)]
            scan(T.sj[:, k - w // 2:k], t[:, c % 4:2 * w:4], t[:, 2 * w + c % 4:4 * w:4], float(-w), A.add, A.add,
                 ["c%d" % c], ["sj%d" % c])

        def row(c):
            out, name = dest(c)
            ts(out, row_v(WIDTH[c]), scalar(c), 2.0, A.is_lt, A.mult, res_k(c) + res_v[0], [name] + res_v[1])

        order = list(range(23 - nv, -1, -1))
        if narrow_first:
            order = [11, 10] + [c for c in order if c not in (11, 10)]
        for c in order:
            out, name = dest(c)
            act(out, row_s(WIDTH[c]), F.Sign, res_k(c) + res_s[0], [name, "aw%d" % c] + res_s[1], bias=scalar(c), scale=-1.0,
                accum=sm("aw", c, c + 1))
        row(23)
        for f in early:
            f()
        for c in range(22, 19, -1):
            row(c)
        todo = list(range(23, 23 - nv, -1))
        if nv > 4:
            row(19)
            cols_of(5, True)
            for c in range(18, 23 - nv, -1):
                row(c)
            for f in later[:1]:
                f()
            sums(todo.pop(0))
        else:
            for f in later[:1]:
                f()
            cols_of(5, True)
        cols_of(4, False)
        for f in later[1:2]:
            f()
        cols_of(3, False)
        for f in later[2:]:
            f()
        cols_of(2, False)
        for c in todo[:3]:
            sums(c)
        k = 192 * (24 - nv - 16) + 191
        latch(T.colw[:], T.mp[:, 0:320], T.p5[:, 0:320], mp, ["colw", "p5"])
        for c in todo[3:]:
            sums(c)
        ts(sm("cw2", 0, 16), T.colw[:, 15:256:16], col(CB), 16.0 * nv, A.subtract, A.add, ["colw", "cb"], ["cw2a"])
        ts(sm("cw2", 16, 20), T.colw[:, 271:320:16], col(CB), 64.0, A.subtract, A.add, ["colw", "cb"], ["cw2b"])
        ts(sm("aw", 24 - nv, 24), T.sj[:, k:8 * 192:192], 1.0, None, A.add, None,
           ["sj%d" % c for c in range(24 - nv, 24)], ["aw%d" % c for c in range(24 - nv, 24)])
        for f in last:
            f()
        tt(sm("tau"), sm("aw"), sm("cw2"), A.add, ["aw%d" % c for c in range(24)] + ["cw2a", "cw2b", "cw2z"], ["tau"])

    for r in range(R):
        wn, xt, tq = T["wn%d" % r], T["xt%d" % r], "tq%d" % r
        tn = state(r)
        dst, src = T.cores[(rank + STEP[r]) % n], T.cores[(rank - STEP[r]) % n]
        qt, ql = "t%d" % r, "l%d" % r
        quant_halves(qt, wn, tn)
        send(dst, "aq%d" % r, T["Q" + ql][:].bitcast(dt.uint8), T["Q" + qt][:].bitcast(dt.uint8), [qt + "0", qt + "1"])
        send(dst, "aq%d" % r, T["Z" + ql][:], T["Z" + qt][:], [qt + "0", qt + "1"])
        arrive(src, "aq%d" % r, 2, ["Q" + ql, "Z" + ql])
        if r == 0:
            late_tables()
        mm_half("p7", "us", qt, 1)
        mm_half("p6", "us", qt, 0)
        mm("p2", "u", 0, qt, C)
        mm("p0", "us", 0, qt, C)
        mm("p1", "us", 0, qt, C)
        if r == 0:
            quant("k", T.wt[:], 384, w1 + ["wb", "wp"])
        tt(T.mk[:, H:C], T.p7[:, 0:H], T.mask[:], A.mult, ["mask"], ["mk1", "p7"])
        tt(T.mk[:, 0:H], T.p6[:, 0:H], T.mask[:], A.mult, ["mask"], ["mk0", "p6"])
        for h in (1, 0):
            scan(T.sw[:, H * h:H * h + H], T.nmask[:], T.mk[:, H * h:H * h + H], 0.0, A.mult, A.add, ["nmask", "mk%d" % h], ["sw%d" % h])

        def homes():
            quant("h", T.hb[:], C, ["hb"])
            mm("p4", "k", 256, "h", C)
            mm("p3", "k", 128, "h", C)

        def home_keys():
            latch(T.hw[:], T.mp[:], T.p4[:, 0:C], mp, ["hw", "p4"])
            tt(T.brow[:], T.p3[:, 0:C], T.iob[:], A.add, ["iob"], ["brow", "p3"])
            ts(sm("bw"), T.hw[:, wrap], col(CB), 0.25, A.subtract, A.mult, ["hw", "cb"], ["bw"])

        def home_wrap():
            tt(sm("bw2"), sm("bw"), sm("ck"), A.add, ["bw", "ck"], ["bw2"])

        def packed():
            tt(T.prow[:], T.p4[:, 0:C], T.iok[:], A.add, ["iok"], ["prow", "p4"])

        def key_base():
            tt(sm("bc"), sm("bw2"), sm("cw2"), A.subtract, ["bw2", "cw2a", "cw2b", "cw2z"], ["bc"])

        act(T.hb[:, 0:4 * C:4], T.p2[:, 0:C], F.Sign, [], ["hb", "p2"], bias=-TINY)
        ranking(NV[0], lambda w: T.p0[:, 0:w], lambda w: T.p1[:, 0:w], ([], ["p0"]), ([], ["p1"]),
                lambda c: T.sw[:, 16 * c + 15:16 * c + 16], lambda c: ["sw%d" % (c // 12)], [homes],
                [home_keys, packed, home_wrap], [key_base])
        tt(sm("kw"), sm("bc"), sm("aw"), A.subtract, ["bc"] + ["aw%d" % c for c in range(24)], ["kw"])
        ts(T.o1[:], sm("tau"), -1.0, 383.0, A.mult, A.add, ["tau"], ["o1"])
        if r == 0:
            ts(T.v4a[:], T.v4[:], 2, 3, A.arith_shift_right, A.bitwise_and, ["v4"], ["v4a"])
        for h in range(2):
            tt(T.krow[:, H * h:H * h + H], T.iop[:].indirect(T.o1[:, 12 * h:12 * h + 12]), T.brow[:, H * h:H * h + H], A.add,
               ["iop", "o1", "brow"], ["krow%d" % h])
        if r == 0:
            ts(T.m4[:, L:2 * L], T.v4a[:], 0.0, -6 * B, A.is_equal, A.mult, ["v4a"], ["m4a"])
        banks = ["p2", "p6", "p7", "p0"]

        def unpack():
            for b in range(4):
                mm(banks[b], "e", 128 * b, ql, C)

        def ident(b):
            op("V", lambda e: e.quantize_mx(T.Qe[:, 128 * b:128 * b + 128], T.Ze[:, 128 * b:128 * b + 128],
                                            T.et[:, 512 * b:512 * b + 512]), ["et%d" % b], ["Qe%d" % b] + (["Qe", "Ze"] if b == 3 else []))

        if r > 0:
            unpack()
        ranking(NV[1], lambda w: T.krow[:, 0:w], lambda w: T.krow[:, 0:w], ([], []), ([], []), lambda c: sm("kw", c, c + 1),
                lambda c: ["kw", "krow0"] + (["krow1"] if WIDTH[c] > H else []), [], [], [], True)
        if r == 0:
            ident(0)
        ts(T.o2[:], sm("tau"), 383.0, 0.5, A.add, A.mult, ["tau"], ["o2"])
        if r == 0:
            ident(1)
        cp(T.ps[:].indirect(T.o2[:]), T.prow[:], ["prow", "o2"], ["ps"])
        if r == 0:
            ident(2)
            for h in range(2):
                act(T.mc[:, H * h:H * h + H], T.mask[:], F.Identity, ["mask"], ["mc%d" % h], bias=BC, scale=-18 * BC)
            act(T.m4[:, 0:L], T.m4[:, L:2 * L], F.Identity, ["m4a"], ["m4"], bias=B)
        scan(T.qs[:], T.c1k[:], T.ps[:], -4096.0, A.add, A.max, ["c1k", "ps"], ["qs"])
        if r == 0:
            ident(3)
            unpack()
        for b in range(4):
            acopy(T.dw[:, b:4 * C:4], T[banks[b]][:, 0:C], [], ["dw%d" % b, banks[b]])
        latch(T.qw[:], T.mp[:], T.qs[:], mp + ["qs"], ["qw"])
        if r == 0:
            ts(T.pki[:, 8:9], T.v4[:, 0:1], 3, None, A.bitwise_and, None, ["v4"], ["ti"])
            ts(col(CB4), T.v4a[:, 3:4], B, None, A.mult, None, ["v4a"], ["cb4"])
        ts(T.oq[:], T.qw[:, wrap], col(CB), 1 / 1024, A.subtract, A.mult, ["qw", "cb"], ["oq"])
        if r == 0:
            ts(col(TC), T.pki[:, 8:9], -1.0, 3.0, A.mult, A.add, ["ti"], ["tc"])
        cp(xt[:, C:3 * C].indirect(T.oq[:]), T.ps[:], ["ps", "oq"], [tq])
        act(T.tr1[:], xt[:, C:3 * C], F.Identity, [tq], ["tr1"], bias=MAGIC)
        act(T.tr2[:, 0:C], T.tr1[:, 0:C], F.Identity, ["tr1"], ["tr2a"], bias=-MAGIC / 2, scale=0.5)
        act(T.tr2[:, C:2 * C], T.tr1[:, C:2 * C], F.Identity, ["tr1"], ["tr2b"], bias=-MAGIC / 2 - 384 * 512, scale=0.5)
        latch(T.xw[:, C:2 * C], T.mc[:], xt[:, C:2 * C], mc + [tq], ["xwb"])
        scan(xt[:, 0:C], xt[:, C:2 * C], T.c1k[:], 383.125 * EMPTY, A.add, A.max, [tq, "c1k"], ["cum%d" % r])
        ts(sm("la"), T.xw[:, C + 15:2 * C:16], col(CBC), 1024.0, A.subtract, A.mult, ["xwb", "cbc"], ["la"])
        latch(T.xw[:, 0:C], T.mc[:], xt[:, 0:C], mc + ["cum%d" % r], ["xwa"])
        tt(sm("lb"), sm("la"), sm("ce"), A.add, ["la", "ce"], ["lb"])
        tt(sm("lc"), sm("lb"), T.xw[:, wrap], A.min, ["lb", "xwa"], ["lc"])
        ts(T.ol[:], sm("lc"), col(CBC), 1 / EMPTY, A.subtract, A.mult, ["lc", "cbc"], ["ol"])
        tt(T.k3[:], T.tr2[:].indirect(T.ol[:]), T.k3c[:], A.add, ["tr2a", "tr2b", "ol", "k3c"], ["k3"])
        acopy(T.grow[:], xt[:, C:3 * C].indirect(T.ol[:]), [tq, "ol"], ["grow"])
        latch(T.k3s[:], T.mp[:], T.k3[:], mp + ["k3"], ["k3s"])
        act(T.k3r[:], T.k3[:], F.Identity, ["k3", "cb"], ["k3r"], bias=col(CB))
        ranking(NV[2], lambda w: T.k3r[:, 0:w], lambda w: T.k3r[:, 0:w], (["k3r"], []), (["k3r"], []),
                lambda c: T.k3s[:, 16 * c + 15:16 * c + 16], lambda c: ["k3s"], [], [], [])
        ts(T.o3[:], sm("tau"), 383.0, 0.5, A.add, A.mult, ["tau"], ["o3"])
        ts(sm("fa"), sm("tau"), -191.0, None, A.is_lt, None, ["tau"], ["fa"])
        cp(T.bl[:].indirect(T.o3[:]), T.grow[:], ["grow", "o3"], ["bl"])
        ts(sm("fb"), sm("tau"), 1151.0, 0.5, A.add, A.mult, ["tau"], ["fb"])
        latch(T.b4[:], T.m4[:, 0:L], T.bl[:, 0:L], ["m4", "bl"], ["b4"])
        ts(si(0), T.b4[:, 3:L:4], col(CB4), None, A.subtract, None, ["b4", "cb4"], ["bi"])
        ts(si(1), si(0), 1023, None, A.bitwise_and, None, ["bi"], ["bj"])
        ob, oa = T["ob%d" % r], T["oa%d" % r]
        ts(ob[:], si(1), 4.0, col(TC), A.mult, A.add, ["bj", "tc"], ["ob%d" % r])
        send(dst, "ao%d" % r, oa[:], ob[:], ["ob%d" % r])
        arrive(src, "ao%d" % r, 1, ["oa%d" % r])
        latch(T.gw[:], T.mp[:], T.grow[:], mp + ["grow"], ["gw"])
        tt(sm("fc"), sm("fa"), sm("fb"), A.mult, ["fa", "fb"], ["fc"])
        ts(si(2), T.gw[:, wrap], col(CB), None, A.subtract, None, ["gw", "cb"], ["mi"])
        ts(si(3), si(2), 1023, None, A.bitwise_and, None, ["mi"], ["mj"])
        tt(sm("idx"), si(3), sm("fc"), A.max, ["mj", "fc"], ["idx"])
        for t in range(4):
            ts(T.ov[:, 24 * t:24 * t + 24], sm("idx"), 4.0, float(t), A.mult, A.add, ["idx"], ["ov%d" % t])
        if r == R - 1:
            cp(T.oo[:], sm("idx"), ["idx"], ["oo"])
            acopy(T.otr[:], T.iop[:].indirect(T.oo[:]), ["iop", "oo"], ["otr"])
            for k in range(8):
                dma("Y", "dot", T.ot[k:k + 1, :], T.otr[16 * k:16 * k + 1, :], ["otr"], [])
            quant("v", T.vt[:], 128, ["vt"])
        dws = ["dw%d" % b for b in range(4)]
        cp(wn[:, 4 * C:4 * C + 192], T.dw[:].indirect(oa[:, 0:12]), dws + ["oa%d" % r], ["Ba%d" % r])
        acopy(wn[:, 4 * C + 192:4 * C + 384], T.dw[:].indirect(oa[:, 12:24]), dws + ["oa%d" % r], ["Bb%d" % r])
        win = tn + ["Ba%d" % r, "Bb%d" % r]
        for t in range(4):
            (cp if t < 2 else acopy)(T.vv[:, t:4 * C:4], wn[:].indirect(T.ov[:, 24 * t:24 * t + 24]), win + ["ov%d" % t], ["vv%d" % t])
        quant_halves("m", T.vv, ["vv0", "vv1", "vv2", "vv3", "vv3"])
        ts(T.v64[:, 0:C], T.vv[:, 0:4 * C:4], 64.0, None, A.mult, None, ["vv0"], ["v640"])
        mm_half("p5", "lay", "m", 1)
        mm_half("p2", "lay", "m", 0)
        rb = ["p0", "p1", "p3", "p4"]
        for b in (3, 1, 2):
            mm(rb[b], "lay", 128 * b, "m", C)
        for b in (2, 1):
            act(T.v64[:, C * b:C * b + C], T.vv[:, b:4 * C:4], F.Identity, ["vv%d" % b], ["v64%d" % b], scale=64.0)
        act(T.tmp[:, 3 * C:4 * C], T.p4[:, 0:C], F.Identity, [], ["tmp3", "p4"], scale=0.015625)
        new = T["wn%d" % (r + 1)] if r + 1 < R else T.tf
        for b in range(3):
            if b == 0:
                tt(T.tmp[:, H:C], T.p5[:, 0:H], T.v64[:, H:C], A.add, ["v640"], ["tmp0h", "p5"])
                tt(T.tmp[:, 0:H], T.p2[:, 0:H], T.v64[:, 0:H], A.add, ["v640"], ["tmp0", "p2"])
            else:
                tt(T.tmp[:, C * b:C * b + C], T[rb[b]][:, 0:C], T.v64[:, C * b:C * b + C], A.add, ["v64%d" % b], ["tmp%d" % b, rb[b]])
            act(new[:, b:4 * C:4], T.tmp[:, C * b:C * b + C], F.Identity, ["tmp%d" % b, "tmp0h"], ["T%d_%d" % (r + 1, b)], scale=0.015625)
        for h in (1, 0):
            tt(new[:, 4 * H * h + 3:4 * H * h + 4 * H:4], T.tmp[:, 3 * C + H * h:3 * C + H * h + H],
               T.vv[:, 4 * H * h + 3:4 * H * h + 4 * H:4], A.add, ["tmp3", "vv3"], ["T%d_3%d" % (r + 1, h)])

    quant_halves("f", T.tf, state(R))
    mm_half("p7", "v", "f", 1)
    mm_half("p6", "v", "f", 0)
    dma("Y", "doa", T.oc[:], T.Qf[:].bitcast(dt.uint8), ["f0", "f1"], [])
    cp(T.yo[:, H:C], T.p7[:, 0:H], [], ["yb", "p7"])
    cp(T.yo[:, 0:H], T.p6[:, 0:H], [], ["ya", "p6"])
    for k in range(4):
        dma("S" if k < 2 else "Y", "dob" if k < 2 else "doa", T.osc[4 * k:4 * k + 4, :], T.Zf[32 * k:32 * k + 4, :], ["f0", "f1"], [])
    dma("S", "dob", T.y[:, H:C], T.yo[:, H:C], ["yb"], [])
    dma("Y", "doa", T.y[:, 0:H], T.yo[:, 0:H], ["ya"], [])
    _emit(g, T, ops)
